import numpy as np
import ml_dtypes


def mxq(x, axis, fmt="e4m3"):
    dtype, down = {"e4m3": (ml_dtypes.float8_e4m3fn, 7), "e5m2": (ml_dtypes.float8_e5m2, 14)}[fmt]
    v = np.moveaxis(np.asarray(x, np.float32).astype(ml_dtypes.bfloat16).astype(np.float64), axis, -1)
    blocks = v.reshape(v.shape[:-1] + (-1, 32))
    amax = np.abs(blocks).max(-1, keepdims=True)
    byte = np.maximum(np.where(amax > 0, np.frexp(amax)[1] - 1 + 127, 0) - down, 1)
    scale = np.exp2(byte - 127.0)
    codes = (blocks / scale).astype(np.float32).astype(dtype).astype(np.float64)
    return np.moveaxis((codes * scale).reshape(v.shape), -1, axis)


WIDE = False


def mx_kscale(k):
    if not WIDE:
        return np.ones(k)
    levels = np.array([10, -10, 5, -5, 0])
    if k % 512:
        return np.exp2(np.random.permutation(np.resize(levels, k // 32))).repeat(32)
    a = np.empty((k // 512, 16))
    for p in range(k // 512):
        a[p, :8] = np.random.permutation(np.resize(levels, 8))
        for g in range(8):
            far = levels[np.abs(levels - a[p, g]) >= 10]
            a[p, g + 8] = far[np.random.randint(len(far))]
    return np.exp2(a.ravel()).repeat(32)


def f64(x):
    return np.asarray(x).astype(np.float64)


def striped(idx):
    return np.tile(idx.reshape(-1, 16).T, (8, 1)).astype(np.uint16)


def unstriped(offs):
    return offs[:16].T.reshape(-1).astype(np.int64)


E2M1 = np.array([0.0, 0.5, 1.0, 1.5, 2.0, 3.0, 4.0, 6.0, -0.0, -0.5, -1.0, -1.5, -2.0, -3.0, -4.0, -6.0])


def pack_weight(w, fmt):
    k, n = w.shape
    w = f64(np.asarray(w, np.float32).astype(ml_dtypes.bfloat16)).reshape(k // 32, 32, n)
    amax = np.abs(w).max(1)
    if fmt == "e4m3":
        byte = np.frexp(amax)[1] - 1 + 127 - 7
    else:
        mant, ex = np.frexp(amax / 6.0)
        byte = np.where(mant > 0.5, ex, ex - 1) + 127
    byte = np.clip(np.where(amax > 0, byte, 1), 1, 254)
    scaled = (w * np.exp2(127.0 - byte)[:, None, :]).reshape(k, n).astype(np.float32)
    by_word = np.ascontiguousarray(scaled.reshape(k // 512, 128, 4, n).transpose(0, 1, 3, 2))
    if fmt == "e4m3":
        words = by_word.astype(ml_dtypes.float8_e4m3fn).view(np.uint8)
    else:
        c = by_word.astype(ml_dtypes.float4_e2m1fn).view(np.uint8) & 0xF
        words = (c[..., 0::2] | (c[..., 1::2] << 4)).reshape(k // 512, 128, 2 * n)
    return np.ascontiguousarray(words), np.ascontiguousarray(byte.astype(np.uint8).reshape(k // 512, 16, n))


def unpack_weight(words, scales, fmt):
    g, _, n = scales.shape
    words = np.ascontiguousarray(words).reshape(g, 128, n, -1)
    if fmt == "e4m3":
        vals = words.view(ml_dtypes.float8_e4m3fn).astype(np.float64)
    else:
        nib = np.empty((g, 128, n, 4), np.uint8)
        nib[..., 0::2] = words & 0xF
        nib[..., 1::2] = words >> 4
        vals = E2M1[nib]
    vals = vals * np.repeat(np.exp2(scales.astype(np.float64) - 127.0), 8, axis=1)[..., None]
    return vals.transpose(0, 1, 3, 2).reshape(g * 512, n)


def gelu(v):
    return 0.5 * v * (1.0 + np.tanh(np.sqrt(2.0 / np.pi) * (v + 0.044715 * v**3)))


K, T, E, C, H, N = 512, 384, 12, 128, 512, 256
TOP = 4


def by_expert(wq, xq):
    return np.concatenate([wq[e].T @ xq[:, e * C:(e + 1) * C] for e in range(E)], axis=1)


def setup_inputs():
    n = np.random.standard_normal
    s = mx_kscale(K)[:, None]
    u = mx_kscale(H)
    deal = np.repeat(np.arange(E), C).reshape(TOP, T)[:, np.random.permutation(T)]
    deal = np.take_along_axis(deal, np.argsort(np.random.rand(TOP, T), axis=0), axis=0)
    for _ in range(8):
        s_, t_ = np.random.permutation(T).reshape(2, -1); r = np.random.randint(TOP, size=T // 2); x, y = deal[r, s_].copy(), deal[r, t_].copy()
        ok = ~((deal[:, s_] == y).any(0) | (deal[:, t_] == x).any(0)); deal[r[ok], s_[ok]] = y[ok]; deal[r[ok], t_[ok]] = x[ok]
    order = np.lexsort((np.random.rand(TOP * T), deal.reshape(-1)))
    slot_token = order % T; pos = np.empty(TOP * T, np.int64); pos[order] = np.arange(TOP * T); pos = pos.reshape(TOP, T)
    g = np.random.uniform(0.5, 1.5, (TOP, T)); g = g / g.sum(0)
    w1 = [pack_weight(m, "e2m1") for m in n((E, K, H)) / np.sqrt(K) / s[None]]
    w3 = [pack_weight(m, "e2m1") for m in n((E, K, H)) / np.sqrt(K) / s[None] * u[None, None, :]]
    w2 = [pack_weight(m, "e2m1") for m in n((E, H, N)) / np.sqrt(H) / u[None, :, None]]
    return {
        "xT": (n((K, T)) * s).astype(np.float32),
        "w1_words": np.stack([m[0] for m in w1]),
        "w1_scales": np.stack([m[1] for m in w1]),
        "w3_words": np.stack([m[0] for m in w3]),
        "w3_scales": np.stack([m[1] for m in w3]),
        "w2_words": np.stack([m[0] for m in w2]),
        "w2_scales": np.stack([m[1] for m in w2]),
        "gate": np.stack([np.tile(r, (N, 1)) for r in g]).astype(np.float32),
        "offs": striped(slot_token),
        "pos1": striped(pos[0]),
        "pos2": striped(pos[1]),
        "pos3": striped(pos[2]),
        "pos4": striped(pos[3]),
    }


def reference(xT, w1_words, w1_scales, w3_words, w3_scales, w2_words, w2_scales, gate, offs, pos1, pos2, pos3, pos4):
    idx = unstriped(offs)
    w1 = np.stack([unpack_weight(w1_words[e], w1_scales[e], "e2m1") for e in range(E)])
    w3 = np.stack([unpack_weight(w3_words[e], w3_scales[e], "e2m1") for e in range(E)])
    w2 = np.stack([unpack_weight(w2_words[e], w2_scales[e], "e2m1") for e in range(E)])
    xq = mxq(f64(xT)[:, idx], 0, "e4m3")
    h = gelu(by_expert(w1, xq))
    h = h * by_expert(w3, xq)
    y = by_expert(w2, mxq(h, 0, "e4m3"))
    return sum(f64(gate[r]) * y[:, unstriped(p)] for r, p in enumerate((pos1, pos2, pos3, pos4)))

@@ -1,0 +1,272 @@
+from contextlib import ExitStack
+
+import concourse.mybir as mybir
+from concourse.masks import make_identity
+
+K, T, E, C, H, N = 512, 384, 12, 128, 512, 256
+TOP = 4
+S = E * C
+P = 128
+HALVES = N // P
+WINDOW = 512
+
+FLOPS = 2 * S * (2 * K * H + H * N)
+
+F32 = mybir.dt.float32
+BF16 = mybir.dt.bfloat16
+I32 = mybir.dt.int32
+U32 = mybir.dt.uint32
+U16 = mybir.dt.uint16
+U8 = mybir.dt.uint8
+FP8X4 = mybir.dt.float8_e4m3fn_x4
+FP4X4 = mybir.dt.float4_e2m1fn_x4
+GELU = mybir.ActivationFunctionType.Gelu_apprx_tanh
+ADD, MULT = mybir.AluOpType.add, mybir.AluOpType.mult
+
+GATHER_GROUPS = [(0, 1), (1, 2), (2, 4), (4, 6), (6, 8), (8, 10), (10, 12)]
+WORD_GROUPS = [(2, 4), (4, 6), (6, 9), (9, 12)]
+X_CHUNKS = [(0, 256, 160), (256, 384, 80)]
+
+
+def tile_moe_tk_glu_gelu_kernel(
+    tc, xT, w1_words, w1_scales, w3_words, w3_scales, w2_words, w2_scales, gate, offs, pos1, pos2, pos3, pos4, out
+):
+    nc = tc.nc
+    with ExitStack() as ctx:
+        lists = ctx.enter_context(tc.tile_pool(name="lists", bufs=1))
+        keep = ctx.enter_context(tc.tile_pool(name="keep", bufs=1))
+        ring = ctx.enter_context(tc.tile_pool(name="ring", bufs=3))
+        pair = ctx.enter_context(tc.tile_pool(name="pair", bufs=3))
+        psum = ctx.enter_context(tc.psum_pool(name="psum", bufs=2))
+
+        offs_t = lists.tile([P, S // 16], U16, name="offs_t")
+        pos_t = [lists.tile([P, T // 16], U16, name=f"pos_t{r}") for r in range(TOP)]
+
+        s1 = keep.tile([P, E, H], U8, name="s1", align_bytes=64)
+        s3 = keep.tile([P, E, H], U8, name="s3", align_bytes=64)
+        s2 = keep.tile([P, E, N], U8, name="s2", align_bytes=64)
+        w1 = keep.tile([P, E, 2 * H], U8, name="w1", align_bytes=64)
+        w3 = keep.tile([P, E, 2 * H], U8, name="w3", align_bytes=64)
+        w2 = keep.tile([P, E, 2 * N], U8, name="w2", align_bytes=64)
+        gate_t = keep.tile([P, TOP, HALVES, T], F32, name="gate_t", align_bytes=64)
+        codes = keep.tile([P, WINDOW], I32, name="codes", align_bytes=64)
+        cscale = keep.tile([P, WINDOW], U8, name="cscale", align_bytes=64)
+        ident = keep.tile([P, P], F32, name="ident", align_bytes=64)
+        warm = keep.tile([P, 1], F32, name="warm")
+        y = [keep.tile([P, S], F32, name=f"y{h}", align_bytes=64) for h in range(HALVES)]
+        prod = keep.tile([P, TOP, HALVES, T], F32, name="prod", align_bytes=64)
+
+        nc.vector.memset(warm[:], 0.0)
+        nc.vector.memset(codes[:, T:WINDOW], 0)
+        nc.gpsimd.memset(cscale[:], 0)
+        make_identity(nc, ident[:])
+        warm_out = keep.tile([P, 1], F32, name="warm_out")
+        nc.scalar.activation(warm_out[:], warm[:], GELU)
+
+        def load_words(tile, words, a, b):
+            nc.sync.dma_start(
+                out=tile[:, a:b, :].bitcast(I32),
+                in_=words[a:b, 0, :, :].rearrange("e p n -> p e n").bitcast(I32),
+            )
+
+        def load_scales(tile, scales):
+            for q in range(4):
+                nc.sync.dma_start(
+                    out=tile[32 * q : 32 * q + 4, :, :].bitcast(I32),
+                    in_=scales[:, 0, 4 * q : 4 * q + 4, :].rearrange("e q n -> q e n").bitcast(I32),
+                )
+
+        x_rows = xT.rearrange("(p j) w -> p j w", j=4)
+        raw = []
+        for i, (a, b, split) in enumerate(X_CHUNKS):
+            chunk = keep.tile([P, 4, b - a], F32, name=f"raw{i}", align_bytes=64)
+            nc.sync.dma_start(out=chunk[:], in_=x_rows[:, :, a:b])
+            raw.append(chunk)
+        nc.sync.dma_start(offs_t[:], offs)
+        load_scales(s1, w1_scales)
+        load_words(w1, w1_words, 0, 1)
+        load_scales(s3, w3_scales)
+        load_words(w3, w3_words, 0, 1)
+        load_words(w1, w1_words, 1, 2)
+        load_words(w3, w3_words, 1, 2)
+        load_words(w2, w2_words, 0, 2)
+        load_scales(s2, w2_scales)
+        for a, b in WORD_GROUPS:
+            load_words(w1, w1_words, a, b)
+            load_words(w3, w3_words, a, b)
+            load_words(w2, w2_words, a, b)
+        for r, pos in enumerate((pos1, pos2, pos3, pos4)):
+            nc.sync.dma_start(pos_t[r][:], pos)
+        nc.sync.dma_start(
+            out=gate_t[:].rearrange("p r h t -> p (r h) t"),
+            in_=gate.rearrange("r n t -> (r n) t").rearrange("(g p) t -> p g t", p=P),
+        )
+
+        for i, (a, b, split) in enumerate(X_CHUNKS):
+            grouped = keep.tile([P, b - a, 4], BF16, name=f"grouped{i}", align_bytes=64)
+            turned = raw[i][:].rearrange("p j w -> p w j")
+            nc.vector.tensor_copy(out=grouped[:, :split, :], in_=turned[:, :split, :])
+            nc.scalar.copy(out=grouped[:, split:, :], in_=turned[:, split:, :])
+            nc.vector.quantize_mx(
+                out=codes[:, a:b].bitcast(FP8X4),
+                scales=cscale[:, a:b],
+                in_=grouped[:].rearrange("p w j -> p (w j)"),
+            )
+
+        slot_words = {}
+        slot_scales = {}
+        live = {}
+
+        def gather(g):
+            a, b = GATHER_GROUPS[g]
+            width = (b - a) * C
+            where = offs_t[:, a * C // 16 : b * C // 16]
+            gs = pair.tile([P, width], U8, name="gs", align_bytes=64)
+            nc.vector.tensor_copy(gs[:], cscale[:].indirect(where))
+            gw = pair.tile([P, width], U32, name="gw", align_bytes=64)
+            nc.vector.tensor_copy(gw[:], codes[:].bitcast(U32).indirect(where))
+            for e in range(a, b):
+                cols = slice((e - a) * C, (e - a + 1) * C)
+                slot_words[e] = gw[:, cols]
+                slot_scales[e] = gs[:, cols]
+
+        def first_layer(e):
+            pa = psum.tile([P, H], F32, name="pa")
+            pb = psum.tile([P, H], F32, name="pb")
+            for bank, words, scales in ((pa, w1, s1), (pb, w3, s3)):
+                nc.tensor.matmul_mx(
+                    out=bank[:],
+                    lhsT=slot_words[e].bitcast(FP8X4),
+                    lhsT_scale=slot_scales[e],
+                    rhs=words[:, e, :].bitcast(FP4X4),
+                    rhs_scale=scales[:, e, :],
+                    start=True,
+                    stop=True,
+                )
+            live[e] = (pa, pb)
+
+        def activate(e):
+            pa, pb = live[e]
+            g = ring.tile([P, H], F32, name="g", align_bytes=64)
+            nc.scalar.activation(
+                out=g[:].rearrange("p (u m e) -> p u m e", u=2, e=2),
+                in_=pa[:].rearrange("p (m u e) -> p u m e", u=2, e=2),
+                func=GELU,
+            )
+            live[e] = (g, pb)
+
+        def multiply(e):
+            g, pb = live[e]
+            h = ring.tile([P, H], BF16, name="h", align_bytes=64)
+            nc.vector.tensor_tensor(
+                out=h[:].rearrange("p (u m e) -> p u m e", u=2, e=2),
+                in0=pb[:].rearrange("p (m u e) -> p u m e", u=2, e=2),
+                in1=g[:].rearrange("p (u m e) -> p u m e", u=2, e=2),
+                op=MULT,
+            )
+            live[e] = h
+
+        def turn(e):
+            h = live[e]
+            pt = psum.tile([P, 2, C], F32, name="pt")
+            words = h[:].bitcast(F32)
+            for u in range(2):
+                nc.tensor.transpose(pt[:, u, :], words[:, u * P : (u + 1) * P], ident[:])
+            live[e] = pt
+
+        def turn_out(e):
+            pt = live[e]
+            ht = ring.tile([P, 4 * C], BF16, name="ht", align_bytes=64)
+            nc.scalar.copy(
+                out=ht[:].bitcast(F32).rearrange("p (s u) -> p s u", u=2),
+                in_=pt[:].rearrange("p u s -> p s u"),
+            )
+            live[e] = ht
+
+        def quantise(e):
+            ht = live[e]
+            hw = ring.tile([P, C], U32, name="hw", align_bytes=64)
+            hs = ring.tile([P, C], U8, name="hs", align_bytes=64)
+            nc.vector.quantize_mx(out=hw[:].bitcast(FP8X4), scales=hs[:], in_=ht[:])
+            live[e] = (hw, hs)
+
+        banks = {}
+
+        def second_layer(e):
+            hw, hs = live[e]
+            if e % 2 == 0:
+                banks[e // 2] = psum.tile([P, HALVES, 2, C], F32, name="py")
+            py = banks[e // 2]
+            for half in range(HALVES):
+                nc.tensor.matmul_mx(
+                    out=py[:, half, e % 2, :],
+                    lhsT=w2[:, e, 2 * P * half : 2 * P * (half + 1)].bitcast(FP4X4),
+                    lhsT_scale=s2[:, e, P * half : P * (half + 1)],
+                    rhs=hw[:].bitcast(FP8X4),
+                    rhs_scale=hs[:],
+                    start=True,
+                    stop=True,
+                )
+
+        def results(e):
+            py = banks[e // 2]
+            if e >= E - 2:
+                nc.scalar.copy(out=y[0][:, e * C : (e + 1) * C], in_=py[:, 0, e % 2, :])
+                nc.vector.tensor_copy(out=y[1][:, e * C : (e + 1) * C], in_=py[:, 1, e % 2, :])
+            elif e % 2 == 1:
+                for half in range(HALVES):
+                    nc.scalar.copy(
+                        out=y[half][:, (e - 1) * C : (e + 1) * C].rearrange("p (b c) -> p b c", b=2),
+                        in_=py[:, half, :, :],
+                    )
+
+        group_of = {}
+        for g, (a, b) in enumerate(GATHER_GROUPS):
+            group_of[a] = g
+
+        gather(0)
+        first_layer(0)
+        for step in range(E + 2):
+            if step < E:
+                activate(step)
+            if step + 1 < E:
+                if step + 1 in group_of:
+                    gather(group_of[step + 1])
+                first_layer(step + 1)
+            if 0 <= step - 1 < E:
+                turn_out(step - 1)
+            if step < E:
+                multiply(step)
+                turn(step)
+            if 0 <= step - 1 < E:
+                quantise(step - 1)
+                second_layer(step - 1)
+                results(step - 1)
+
+        def fetch(r, half):
+            nc.vector.tensor_tensor(prod[:, r, half, :], y[half][:].indirect(pos_t[r][:]), gate_t[:, r, half, :], MULT)
+
+        def add(half, to, left, right):
+            nc.vector.tensor_tensor(to, left, right, ADD)
+
+        sums = keep.tile([P, HALVES, 3, T], F32, name="sums", align_bytes=64)
+
+        def store(half):
+            nc.sync.dma_start(out=out[half * P : (half + 1) * P, :], in_=sums[:, half, 2, :])
+
+        fetch(0, 0)
+        fetch(1, 0)
+        fetch(2, 0)
+        add(0, sums[:, 0, 0, :], prod[:, 0, 0, :], prod[:, 1, 0, :])
+        fetch(3, 0)
+        add(0, sums[:, 0, 1, :], sums[:, 0, 0, :], prod[:, 2, 0, :])
+        fetch(0, 1)
+        add(0, sums[:, 0, 2, :], sums[:, 0, 1, :], prod[:, 3, 0, :])
+        store(0)
+        fetch(1, 1)
+        fetch(2, 1)
+        add(1, sums[:, 1, 0, :], prod[:, 0, 1, :], prod[:, 1, 1, :])
+        fetch(3, 1)
+        add(1, sums[:, 1, 1, :], sums[:, 1, 0, :], prod[:, 2, 1, :])
+        add(1, sums[:, 1, 2, :], sums[:, 1, 1, :], prod[:, 3, 1, :])
+        store(1)

@@ -24,7 +24,6 @@ GELU = mybir.ActivationFunctionType.Gelu_apprx_tanh
 ADD, MULT = mybir.AluOpType.add, mybir.AluOpType.mult
 
 GATHER_GROUPS = [(0, 1), (1, 2), (2, 4), (4, 6), (6, 8), (8, 10), (10, 12)]
-WORD_GROUPS = [(2, 4), (4, 6), (6, 9), (9, 12)]
 X_CHUNKS = [(0, 256, 160), (256, 384, 80)]
 
 
@@ -48,7 +47,7 @@ def tile_moe_tk_glu_gelu_kernel(
         w1 = keep.tile([P, E, 2 * H], U8, name="w1", align_bytes=64)
         w3 = keep.tile([P, E, 2 * H], U8, name="w3", align_bytes=64)
         w2 = keep.tile([P, E, 2 * N], U8, name="w2", align_bytes=64)
-        gate_t = keep.tile([P, TOP, HALVES, T], F32, name="gate_t", align_bytes=64)
+        gate_t = keep.tile([P, TOP, T], F32, name="gate_t", align_bytes=64)
         codes = keep.tile([P, WINDOW], I32, name="codes", align_bytes=64)
         cscale = keep.tile([P, WINDOW], U8, name="cscale", align_bytes=64)
         ident = keep.tile([P, P], F32, name="ident", align_bytes=64)
@@ -69,11 +68,11 @@ def tile_moe_tk_glu_gelu_kernel(
                 in_=words[a:b, 0, :, :].rearrange("e p n -> p e n").bitcast(I32),
             )
 
-        def load_scales(tile, scales):
-            for q in range(4):
+        def load_scales(tile, scales, a, b):
+            for r in range(4):
                 nc.sync.dma_start(
-                    out=tile[32 * q : 32 * q + 4, :, :].bitcast(I32),
-                    in_=scales[:, 0, 4 * q : 4 * q + 4, :].rearrange("e q n -> q e n").bitcast(I32),
+                    out=tile[r:P:32, a:b, :].bitcast(I32),
+                    in_=scales[a:b, 0, r:16:4, :].rearrange("e q n -> q e n").bitcast(I32),
                 )
 
         x_rows = xT.rearrange("(p j) w -> p j w", j=4)
@@ -83,23 +82,37 @@ def tile_moe_tk_glu_gelu_kernel(
             nc.sync.dma_start(out=chunk[:], in_=x_rows[:, :, a:b])
             raw.append(chunk)
         nc.sync.dma_start(offs_t[:], offs)
-        load_scales(s1, w1_scales)
         load_words(w1, w1_words, 0, 1)
-        load_scales(s3, w3_scales)
         load_words(w3, w3_words, 0, 1)
+        load_scales(s1, w1_scales, 0, 2)
+        load_scales(s3, w3_scales, 0, 2)
         load_words(w1, w1_words, 1, 2)
         load_words(w3, w3_words, 1, 2)
+        load_scales(s2, w2_scales, 0, 5)
         load_words(w2, w2_words, 0, 2)
-        load_scales(s2, w2_scales)
-        for a, b in WORD_GROUPS:
-            load_words(w1, w1_words, a, b)
-            load_words(w3, w3_words, a, b)
-            load_words(w2, w2_words, a, b)
+        load_scales(s1, w1_scales, 2, 5)
+        load_scales(s3, w3_scales, 2, 5)
+        load_words(w1, w1_words, 2, 3)
+        load_words(w3, w3_words, 2, 3)
+        load_words(w1, w1_words, 3, 5)
+        load_words(w3, w3_words, 3, 5)
+        load_words(w2, w2_words, 2, 5)
+        load_scales(s1, w1_scales, 5, 12)
+        load_scales(s3, w3_scales, 5, 12)
+        load_words(w1, w1_words, 5, 7)
+        load_words(w3, w3_words, 5, 7)
+        load_scales(s2, w2_scales, 5, 12)
+        load_words(w2, w2_words, 5, 8)
+        load_words(w1, w1_words, 7, 9)
+        load_words(w3, w3_words, 7, 9)
+        load_words(w1, w1_words, 9, 12)
+        load_words(w3, w3_words, 9, 12)
+        load_words(w2, w2_words, 8, 12)
         for r, pos in enumerate((pos1, pos2, pos3, pos4)):
             nc.sync.dma_start(pos_t[r][:], pos)
         nc.sync.dma_start(
-            out=gate_t[:].rearrange("p r h t -> p (r h) t"),
-            in_=gate.rearrange("r n t -> (r n) t").rearrange("(g p) t -> p g t", p=P),
+            out=gate_t[:],
+            in_=gate[:, 0:P, :].rearrange("r p t -> p r t"),
         )
 
         for i, (a, b, split) in enumerate(X_CHUNKS):
@@ -244,7 +257,7 @@ def tile_moe_tk_glu_gelu_kernel(
                 results(step - 1)
 
         def fetch(r, half):
-            nc.vector.tensor_tensor(prod[:, r, half, :], y[half][:].indirect(pos_t[r][:]), gate_t[:, r, half, :], MULT)
+            nc.vector.tensor_tensor(prod[:, r, half, :], y[half][:].indirect(pos_t[r][:]), gate_t[:, r, :], MULT)
 
         def add(half, to, left, right):
             nc.vector.tensor_tensor(to, left, right, ADD)

@@ -34,26 +34,20 @@ def tile_moe_tk_glu_gelu_kernel(
     with ExitStack() as ctx:
         lists = ctx.enter_context(tc.tile_pool(name="lists", bufs=1))
         keep = ctx.enter_context(tc.tile_pool(name="keep", bufs=1))
-        ring = ctx.enter_context(tc.tile_pool(name="ring", bufs=3))
+        ring = ctx.enter_context(tc.tile_pool(name="ring", bufs=4))
         pair = ctx.enter_context(tc.tile_pool(name="pair", bufs=3))
         psum = ctx.enter_context(tc.psum_pool(name="psum", bufs=2))
 
         offs_t = lists.tile([P, S // 16], U16, name="offs_t")
         pos_t = [lists.tile([P, T // 16], U16, name=f"pos_t{r}") for r in range(TOP)]
 
-        s1 = keep.tile([P, E, H], U8, name="s1", align_bytes=64)
-        s3 = keep.tile([P, E, H], U8, name="s3", align_bytes=64)
-        s2 = keep.tile([P, E, N], U8, name="s2", align_bytes=64)
-        w1 = keep.tile([P, E, 2 * H], U8, name="w1", align_bytes=64)
-        w3 = keep.tile([P, E, 2 * H], U8, name="w3", align_bytes=64)
-        w2 = keep.tile([P, E, 2 * N], U8, name="w2", align_bytes=64)
         gate_t = keep.tile([P, TOP, T], F32, name="gate_t", align_bytes=64)
         codes = keep.tile([P, WINDOW], I32, name="codes", align_bytes=64)
         cscale = keep.tile([P, WINDOW], U8, name="cscale", align_bytes=64)
         ident = keep.tile([P, P], F32, name="ident", align_bytes=64)
         warm = keep.tile([P, 1], F32, name="warm")
         y = [keep.tile([P, S], F32, name=f"y{h}", align_bytes=64) for h in range(HALVES)]
-        prod = keep.tile([P, TOP, HALVES, T], F32, name="prod", align_bytes=64)
+        prod = [[keep.tile([P, T], F32, name=f"prod{h}{r}", align_bytes=64) for r in range(TOP)] for h in range(HALVES)]
 
         nc.vector.memset(warm[:], 0.0)
         nc.vector.memset(codes[:, T:WINDOW], 0)
@@ -62,18 +56,26 @@ def tile_moe_tk_glu_gelu_kernel(
         warm_out = keep.tile([P, 1], F32, name="warm_out")
         nc.scalar.activation(warm_out[:], warm[:], GELU)
 
-        def load_words(tile, words, a, b):
+        w1, w3, w2, s1, s3, s2 = {}, {}, {}, {}, {}, {}
+
+        def load_words(held, tag, words, a, b):
+            tile = keep.tile([P, b - a, words.shape[3]], U8, name=f"{tag}_{a}", align_bytes=64)
             nc.sync.dma_start(
-                out=tile[:, a:b, :].bitcast(I32),
+                out=tile[:].bitcast(I32),
                 in_=words[a:b, 0, :, :].rearrange("e p n -> p e n").bitcast(I32),
             )
+            for e in range(a, b):
+                held[e] = tile[:, e - a, :]
 
-        def load_scales(tile, scales, a, b):
+        def load_scales(held, tag, scales, a, b):
+            tile = keep.tile([P, b - a, scales.shape[3]], U8, name=f"{tag}_{a}", align_bytes=64)
             for r in range(4):
                 nc.sync.dma_start(
-                    out=tile[r:P:32, a:b, :].bitcast(I32),
+                    out=tile[r:P:32, :, :].bitcast(I32),
                     in_=scales[a:b, 0, r:16:4, :].rearrange("e q n -> q e n").bitcast(I32),
                 )
+            for e in range(a, b):
+                held[e] = tile[:, e - a, :]
 
         x_rows = xT.rearrange("(p j) w -> p j w", j=4)
         raw = []
@@ -82,32 +84,23 @@ def tile_moe_tk_glu_gelu_kernel(
             nc.sync.dma_start(out=chunk[:], in_=x_rows[:, :, a:b])
             raw.append(chunk)
         nc.sync.dma_start(offs_t[:], offs)
-        load_words(w1, w1_words, 0, 1)
-        load_words(w3, w3_words, 0, 1)
-        load_scales(s1, w1_scales, 0, 2)
-        load_scales(s3, w3_scales, 0, 2)
-        load_words(w1, w1_words, 1, 2)
-        load_words(w3, w3_words, 1, 2)
-        load_scales(s2, w2_scales, 0, 5)
-        load_words(w2, w2_words, 0, 2)
-        load_scales(s1, w1_scales, 2, 5)
-        load_scales(s3, w3_scales, 2, 5)
-        load_words(w1, w1_words, 2, 3)
-        load_words(w3, w3_words, 2, 3)
-        load_words(w1, w1_words, 3, 5)
-        load_words(w3, w3_words, 3, 5)
-        load_words(w2, w2_words, 2, 5)
-        load_scales(s1, w1_scales, 5, 12)
-        load_scales(s3, w3_scales, 5, 12)
-        load_words(w1, w1_words, 5, 7)
-        load_words(w3, w3_words, 5, 7)
-        load_scales(s2, w2_scales, 5, 12)
-        load_words(w2, w2_words, 5, 8)
-        load_words(w1, w1_words, 7, 9)
-        load_words(w3, w3_words, 7, 9)
-        load_words(w1, w1_words, 9, 12)
-        load_words(w3, w3_words, 9, 12)
-        load_words(w2, w2_words, 8, 12)
+        load_words(w1, "w1", w1_words, 0, 1)
+        load_scales(s1, "s1", w1_scales, 0, 4)
+        load_words(w3, "w3", w3_words, 0, 1)
+        load_scales(s3, "s3", w3_scales, 0, 4)
+        load_words(w1, "w1", w1_words, 1, 3)
+        load_words(w3, "w3", w3_words, 1, 3)
+        load_words(w2, "w2", w2_words, 0, 3)
+        load_scales(s2, "s2", w2_scales, 0, 12)
+        load_words(w1, "w1", w1_words, 3, 6)
+        load_words(w3, "w3", w3_words, 3, 6)
+        load_scales(s1, "s1", w1_scales, 4, 12)
+        load_scales(s3, "s3", w3_scales, 4, 12)
+        load_words(w2, "w2", w2_words, 3, 12)
+        load_words(w1, "w1", w1_words, 6, 9)
+        load_words(w3, "w3", w3_words, 6, 9)
+        load_words(w1, "w1", w1_words, 9, 12)
+        load_words(w3, "w3", w3_words, 9, 12)
         for r, pos in enumerate((pos1, pos2, pos3, pos4)):
             nc.sync.dma_start(pos_t[r][:], pos)
         nc.sync.dma_start(
@@ -143,23 +136,26 @@ def tile_moe_tk_glu_gelu_kernel(
                 slot_words[e] = gw[:, cols]
                 slot_scales[e] = gs[:, cols]
 
-        def first_layer(e):
-            pa = psum.tile([P, H], F32, name="pa")
-            pb = psum.tile([P, H], F32, name="pb")
-            for bank, words, scales in ((pa, w1, s1), (pb, w3, s3)):
-                nc.tensor.matmul_mx(
-                    out=bank[:],
-                    lhsT=slot_words[e].bitcast(FP8X4),
-                    lhsT_scale=slot_scales[e],
-                    rhs=words[:, e, :].bitcast(FP4X4),
-                    rhs_scale=scales[:, e, :],
-                    start=True,
-                    stop=True,
-                )
-            live[e] = (pa, pb)
+        def first(e, bank, words, scales):
+            nc.tensor.matmul_mx(
+                out=bank[:],
+                lhsT=slot_words[e].bitcast(FP8X4),
+                lhsT_scale=slot_scales[e],
+                rhs=words[e].bitcast(FP4X4),
+                rhs_scale=scales[e],
+                start=True,
+                stop=True,
+            )
 
-        def activate(e):
-            pa, pb = live[e]
+        def first_a(e):
+            pa = psum.tile([P, H], F32, name="pa")
+            first(e, pa, w1, s1)
+            live[e] = pa
+
+        def first_b_and_activate(e):
+            pa = live[e]
+            pb = psum.tile([P, H], F32, name="pb")
+            first(e, pb, w3, s3)
             g = ring.tile([P, H], F32, name="g", align_bytes=64)
             nc.scalar.activation(
                 out=g[:].rearrange("p (u m e) -> p u m e", u=2, e=2),
@@ -213,8 +209,8 @@ def tile_moe_tk_glu_gelu_kernel(
             for half in range(HALVES):
                 nc.tensor.matmul_mx(
                     out=py[:, half, e % 2, :],
-                    lhsT=w2[:, e, 2 * P * half : 2 * P * (half + 1)].bitcast(FP4X4),
-                    lhsT_scale=s2[:, e, P * half : P * (half + 1)],
+                    lhsT=w2[e][:, 2 * P * half : 2 * P * (half + 1)].bitcast(FP4X4),
+                    lhsT_scale=s2[e][:, P * half : P * (half + 1)],
                     rhs=hw[:].bitcast(FP8X4),
                     rhs_scale=hs[:],
                     start=True,
@@ -237,49 +233,53 @@ def tile_moe_tk_glu_gelu_kernel(
         for g, (a, b) in enumerate(GATHER_GROUPS):
             group_of[a] = g
 
-        gather(0)
-        first_layer(0)
-        for step in range(E + 2):
-            if step < E:
-                activate(step)
-            if step + 1 < E:
-                if step + 1 in group_of:
-                    gather(group_of[step + 1])
-                first_layer(step + 1)
-            if 0 <= step - 1 < E:
-                turn_out(step - 1)
-            if step < E:
-                multiply(step)
-                turn(step)
-            if 0 <= step - 1 < E:
-                quantise(step - 1)
-                second_layer(step - 1)
-                results(step - 1)
+        def gather_for(e):
+            if e in group_of:
+                gather(group_of[e])
+
+        STAGES = (gather_for, first_a, first_b_and_activate, multiply, turn, turn_out, quantise, second_layer, results)
+        for step in range(E + len(STAGES) - 1):
+            for lag in reversed(range(len(STAGES))):
+                if 0 <= step - lag < E:
+                    STAGES[lag](step - lag)
+
+        BLOCKS = T // P
 
         def fetch(r, half):
-            nc.vector.tensor_tensor(prod[:, r, half, :], y[half][:].indirect(pos_t[r][:]), gate_t[:, r, :], MULT)
+            nc.vector.tensor_tensor(prod[half][r][:], y[half][:].indirect(pos_t[r][:]), gate_t[:, r, :], MULT)
 
-        def add(half, to, left, right):
-            nc.vector.tensor_tensor(to, left, right, ADD)
+        turned_sum = {}
+        partial = {}
+        TAGS = (("pa", "pa", "pb", "pb"), ("pt", "pt", "py", "py"))
 
-        sums = keep.tile([P, HALVES, 3, T], F32, name="sums", align_bytes=64)
+        def add_turned(r, half):
+            for b in range(BLOCKS):
+                if r == 0:
+                    turned_sum[half, b] = psum.tile([P, P], F32, name=TAGS[half][b])
+                nc.tensor.matmul(
+                    turned_sum[half, b][:],
+                    lhsT=prod[half][r][:, b * P : (b + 1) * P],
+                    rhs=ident[:],
+                    is_transpose=True,
+                    start=(r == 0),
+                    stop=(r == TOP - 2),
+                )
 
-        def store(half):
-            nc.sync.dma_start(out=out[half * P : (half + 1) * P, :], in_=sums[:, half, 2, :])
+        def turn_back(half):
+            partial[half] = psum.tile([P, T], F32, name=TAGS[half][3])
+            for b in range(BLOCKS):
+                staged = keep.tile([P, P], F32, name=f"staged{half}{b}", align_bytes=64)
+                nc.scalar.copy(out=staged[:], in_=turned_sum[half, b][:])
+                nc.tensor.transpose(partial[half][:, b * P : (b + 1) * P], staged[:], ident[:])
 
-        fetch(0, 0)
-        fetch(1, 0)
-        fetch(2, 0)
-        add(0, sums[:, 0, 0, :], prod[:, 0, 0, :], prod[:, 1, 0, :])
-        fetch(3, 0)
-        add(0, sums[:, 0, 1, :], sums[:, 0, 0, :], prod[:, 2, 0, :])
-        fetch(0, 1)
-        add(0, sums[:, 0, 2, :], sums[:, 0, 1, :], prod[:, 3, 0, :])
-        store(0)
-        fetch(1, 1)
-        fetch(2, 1)
-        add(1, sums[:, 1, 0, :], prod[:, 0, 1, :], prod[:, 1, 1, :])
-        fetch(3, 1)
-        add(1, sums[:, 1, 1, :], sums[:, 1, 0, :], prod[:, 2, 1, :])
-        add(1, sums[:, 1, 2, :], sums[:, 1, 1, :], prod[:, 3, 1, :])
-        store(1)
+        for half in range(HALVES):
+            for r in range(TOP - 1):
+                fetch(r, half)
+                add_turned(r, half)
+            turn_back(half)
+        for half in range(HALVES):
+            fetch(TOP - 1, half)
+        for half in range(HALVES):
+            total = keep.tile([P, T], F32, name=f"total{half}", align_bytes=64)
+            nc.vector.tensor_tensor(total[:], partial[half][:], prod[half][TOP - 1][:], ADD)
+            nc.sync.dma_start(out=out[half * P : (half + 1) * P, :], in_=total[:])

@@ -8,6 +8,7 @@ TOP = 4
 S = E * C
 P = 128
 HALVES = N // P
+BLOCKS = T // P
 WINDOW = 512
 
 FLOPS = 2 * S * (2 * K * H + H * N)
@@ -23,8 +24,11 @@ FP4X4 = mybir.dt.float4_e2m1fn_x4
 GELU = mybir.ActivationFunctionType.Gelu_apprx_tanh
 ADD, MULT = mybir.AluOpType.add, mybir.AluOpType.mult
 
-GATHER_GROUPS = [(0, 1), (1, 2), (2, 4), (4, 6), (6, 8), (8, 10), (10, 12)]
+GATHER_GROUPS = [(0, 1), (1, 3), (3, 5), (5, 7), (7, 9), (9, 11), (11, 12)]
+TURN_GROUPS = [(0, 1), (1, 3), (3, 5), (5, 7), (7, 9), (9, 11), (11, 12)]
+RESULT_GROUPS = [(0, 3), (3, 7), (7, 11), (11, 12)]
 X_CHUNKS = [(0, 256, 160), (256, 384, 80)]
+BANKS = {"pa": 2, "pb": 3, "pt": 2, "py": 1}
 
 
 def tile_moe_tk_glu_gelu_kernel(
@@ -35,8 +39,11 @@ def tile_moe_tk_glu_gelu_kernel(
         lists = ctx.enter_context(tc.tile_pool(name="lists", bufs=1))
         keep = ctx.enter_context(tc.tile_pool(name="keep", bufs=1))
         ring = ctx.enter_context(tc.tile_pool(name="ring", bufs=4))
-        pair = ctx.enter_context(tc.tile_pool(name="pair", bufs=3))
-        psum = ctx.enter_context(tc.psum_pool(name="psum", bufs=2))
+        slots = ctx.enter_context(tc.tile_pool(name="slots", bufs=2))
+        psum = ctx.enter_context(tc.psum_pool(name="psum", bufs=1))
+
+        def bank(tag, shape):
+            return psum.tile(shape, F32, name=tag, bufs=BANKS[tag])
 
         offs_t = lists.tile([P, S // 16], U16, name="offs_t")
         pos_t = [lists.tile([P, T // 16], U16, name=f"pos_t{r}") for r in range(TOP)]
@@ -90,23 +97,22 @@ def tile_moe_tk_glu_gelu_kernel(
         load_scales(s3, "s3", w3_scales, 0, 4)
         load_words(w1, "w1", w1_words, 1, 3)
         load_words(w3, "w3", w3_words, 1, 3)
-        load_words(w2, "w2", w2_words, 0, 3)
-        load_scales(s2, "s2", w2_scales, 0, 12)
-        load_words(w1, "w1", w1_words, 3, 6)
-        load_words(w3, "w3", w3_words, 3, 6)
+        load_words(w1, "w1", w1_words, 3, 5)
+        load_words(w3, "w3", w3_words, 3, 5)
         load_scales(s1, "s1", w1_scales, 4, 12)
         load_scales(s3, "s3", w3_scales, 4, 12)
-        load_words(w2, "w2", w2_words, 3, 12)
-        load_words(w1, "w1", w1_words, 6, 9)
-        load_words(w3, "w3", w3_words, 6, 9)
-        load_words(w1, "w1", w1_words, 9, 12)
-        load_words(w3, "w3", w3_words, 9, 12)
+        load_words(w1, "w1", w1_words, 5, 8)
+        load_words(w3, "w3", w3_words, 5, 8)
+        load_scales(s2, "s2", w2_scales, 0, 12)
+        load_words(w2, "w2", w2_words, 0, 6)
+        load_words(w1, "w1", w1_words, 8, 10)
+        load_words(w3, "w3", w3_words, 8, 10)
+        load_words(w1, "w1", w1_words, 10, 12)
+        load_words(w3, "w3", w3_words, 10, 12)
+        load_words(w2, "w2", w2_words, 6, 12)
         for r, pos in enumerate((pos1, pos2, pos3, pos4)):
             nc.sync.dma_start(pos_t[r][:], pos)
-        nc.sync.dma_start(
-            out=gate_t[:],
-            in_=gate[:, 0:P, :].rearrange("r p t -> p r t"),
-        )
+        nc.sync.dma_start(out=gate_t[:], in_=gate[:, 0:P, :].rearrange("r p t -> p r t"))
 
         for i, (a, b, split) in enumerate(X_CHUNKS):
             grouped = keep.tile([P, b - a, 4], BF16, name=f"grouped{i}", align_bytes=64)
@@ -119,26 +125,29 @@ def tile_moe_tk_glu_gelu_kernel(
                 in_=grouped[:].rearrange("p w j -> p (w j)"),
             )
 
-        slot_words = {}
-        slot_scales = {}
-        live = {}
+        slot_words, slot_scales, hidden_words, hidden_scales = {}, {}, {}, {}
+        pa, pb, gelu, hidden, turned_words, regrouped, py = {}, {}, {}, {}, {}, {}, {}
 
-        def gather(g):
-            a, b = GATHER_GROUPS[g]
-            width = (b - a) * C
-            where = offs_t[:, a * C // 16 : b * C // 16]
-            gs = pair.tile([P, width], U8, name="gs", align_bytes=64)
-            nc.vector.tensor_copy(gs[:], cscale[:].indirect(where))
-            gw = pair.tile([P, width], U32, name="gw", align_bytes=64)
-            nc.vector.tensor_copy(gw[:], codes[:].bitcast(U32).indirect(where))
-            for e in range(a, b):
-                cols = slice((e - a) * C, (e - a + 1) * C)
-                slot_words[e] = gw[:, cols]
-                slot_scales[e] = gs[:, cols]
+        def ending(groups, e):
+            return [(a, b) for a, b in groups if b - 1 == e]
 
-        def first(e, bank, words, scales):
+        def gather(e):
+            for a, b in GATHER_GROUPS:
+                if a == e:
+                    width = (b - a) * C
+                    where = offs_t[:, a * C // 16 : b * C // 16]
+                    gs = slots.tile([P, width], U8, name="gs", align_bytes=64)
+                    nc.vector.tensor_copy(gs[:], cscale[:].indirect(where))
+                    gw = slots.tile([P, width], U32, name="gw", align_bytes=64)
+                    nc.vector.tensor_copy(gw[:], codes[:].bitcast(U32).indirect(where))
+                    for x in range(a, b):
+                        cols = slice((x - a) * C, (x - a + 1) * C)
+                        slot_words[x] = gw[:, cols]
+                        slot_scales[x] = gs[:, cols]
+
+        def first(e, to, words, scales):
             nc.tensor.matmul_mx(
-                out=bank[:],
+                out=to[:],
                 lhsT=slot_words[e].bitcast(FP8X4),
                 lhsT_scale=slot_scales[e],
                 rhs=words[e].bitcast(FP4X4),
@@ -147,115 +156,104 @@ def tile_moe_tk_glu_gelu_kernel(
                 stop=True,
             )
 
-        def first_a(e):
-            pa = psum.tile([P, H], F32, name="pa")
-            first(e, pa, w1, s1)
-            live[e] = pa
+        def first_layer(e):
+            pa[e] = bank("pa", [P, H])
+            first(e, pa[e], w1, s1)
+            pb[e] = bank("pb", [P, H])
+            first(e, pb[e], w3, s3)
 
-        def first_b_and_activate(e):
-            pa = live[e]
-            pb = psum.tile([P, H], F32, name="pb")
-            first(e, pb, w3, s3)
-            g = ring.tile([P, H], F32, name="g", align_bytes=64)
+        def activate(e):
+            gelu[e] = ring.tile([P, H], F32, name="g", align_bytes=64)
             nc.scalar.activation(
-                out=g[:].rearrange("p (u m e) -> p u m e", u=2, e=2),
-                in_=pa[:].rearrange("p (m u e) -> p u m e", u=2, e=2),
+                out=gelu[e][:].rearrange("p (u m v) -> p u m v", u=2, v=2),
+                in_=pa[e][:].rearrange("p (m u v) -> p u m v", u=2, v=2),
                 func=GELU,
             )
-            live[e] = (g, pb)
 
         def multiply(e):
-            g, pb = live[e]
-            h = ring.tile([P, H], BF16, name="h", align_bytes=64)
+            hidden[e] = ring.tile([P, H], BF16, name="h", align_bytes=64)
             nc.vector.tensor_tensor(
-                out=h[:].rearrange("p (u m e) -> p u m e", u=2, e=2),
-                in0=pb[:].rearrange("p (m u e) -> p u m e", u=2, e=2),
-                in1=g[:].rearrange("p (u m e) -> p u m e", u=2, e=2),
+                out=hidden[e][:].rearrange("p (u m v) -> p u m v", u=2, v=2),
+                in0=pb[e][:].rearrange("p (m u v) -> p u m v", u=2, v=2),
+                in1=gelu[e][:].rearrange("p (u m v) -> p u m v", u=2, v=2),
                 op=MULT,
             )
-            live[e] = h
 
         def turn(e):
-            h = live[e]
-            pt = psum.tile([P, 2, C], F32, name="pt")
-            words = h[:].bitcast(F32)
-            for u in range(2):
-                nc.tensor.transpose(pt[:, u, :], words[:, u * P : (u + 1) * P], ident[:])
-            live[e] = pt
+            for a, b in ending(TURN_GROUPS, e):
+                pt = bank("pt", [P, b - a, 2, C])
+                for x in range(a, b):
+                    words = hidden[x][:].bitcast(F32)
+                    for u in range(2):
+                        nc.tensor.transpose(pt[:, x - a, u, :], words[:, u * P : (u + 1) * P], ident[:])
+                turned_words[e] = pt
 
         def turn_out(e):
-            pt = live[e]
-            ht = ring.tile([P, 4 * C], BF16, name="ht", align_bytes=64)
-            nc.scalar.copy(
-                out=ht[:].bitcast(F32).rearrange("p (s u) -> p s u", u=2),
-                in_=pt[:].rearrange("p u s -> p s u"),
-            )
-            live[e] = ht
+            for a, b in ending(TURN_GROUPS, e):
+                ht = ring.tile([P, (b - a) * 4 * C], BF16, name="ht", align_bytes=64)
+                nc.scalar.copy(
+                    out=ht[:].bitcast(F32).rearrange("p (x s u) -> p x s u", x=b - a, u=2),
+                    in_=turned_words[e][:].rearrange("p x u s -> p x s u"),
+                )
+                regrouped[e] = ht
 
         def quantise(e):
-            ht = live[e]
-            hw = ring.tile([P, C], U32, name="hw", align_bytes=64)
-            hs = ring.tile([P, C], U8, name="hs", align_bytes=64)
-            nc.vector.quantize_mx(out=hw[:].bitcast(FP8X4), scales=hs[:], in_=ht[:])
-            live[e] = (hw, hs)
+            for a, b in ending(TURN_GROUPS, e):
+                hw = keep.tile([P, (b - a) * C], U32, name=f"hw{a}", align_bytes=64)
+                hs = keep.tile([P, (b - a) * C], U8, name=f"hs{a}", align_bytes=64)
+                nc.vector.quantize_mx(out=hw[:].bitcast(FP8X4), scales=hs[:], in_=regrouped[e][:])
+                for x in range(a, b):
+                    cols = slice((x - a) * C, (x - a + 1) * C)
+                    hidden_words[x] = hw[:, cols]
+                    hidden_scales[x] = hs[:, cols]
 
-        banks = {}
+        def second(e, half, to):
+            nc.tensor.matmul_mx(
+                out=to,
+                lhsT=w2[e][:, 2 * P * half : 2 * P * (half + 1)].bitcast(FP4X4),
+                lhsT_scale=s2[e][:, P * half : P * (half + 1)],
+                rhs=hidden_words[e].bitcast(FP8X4),
+                rhs_scale=hidden_scales[e],
+                start=True,
+                stop=True,
+            )
 
         def second_layer(e):
-            hw, hs = live[e]
-            if e % 2 == 0:
-                banks[e // 2] = psum.tile([P, HALVES, 2, C], F32, name="py")
-            py = banks[e // 2]
-            for half in range(HALVES):
-                nc.tensor.matmul_mx(
-                    out=py[:, half, e % 2, :],
-                    lhsT=w2[e][:, 2 * P * half : 2 * P * (half + 1)].bitcast(FP4X4),
-                    lhsT_scale=s2[e][:, P * half : P * (half + 1)],
-                    rhs=hw[:].bitcast(FP8X4),
-                    rhs_scale=hs[:],
-                    start=True,
-                    stop=True,
-                )
+            for first_x, end_x in ending(TURN_GROUPS, e):
+                for x in range(first_x, end_x):
+                    for a, b in RESULT_GROUPS:
+                        if x == a:
+                            py[a] = bank("pb" if a == E - 1 else "py", [P, (b - a) * C])
+                        if a <= x < b:
+                            second(x, 0, py[a][:, (x - a) * C : (x - a + 1) * C])
 
         def results(e):
-            py = banks[e // 2]
-            if e >= E - 2:
-                nc.scalar.copy(out=y[0][:, e * C : (e + 1) * C], in_=py[:, 0, e % 2, :])
-                nc.vector.tensor_copy(out=y[1][:, e * C : (e + 1) * C], in_=py[:, 1, e % 2, :])
-            elif e % 2 == 1:
-                for half in range(HALVES):
-                    nc.scalar.copy(
-                        out=y[half][:, (e - 1) * C : (e + 1) * C].rearrange("p (b c) -> p b c", b=2),
-                        in_=py[:, half, :, :],
-                    )
+            for a, b in ending(RESULT_GROUPS, e):
+                nc.scalar.copy(out=y[0][:, a * C : b * C], in_=py[a][:])
 
-        group_of = {}
-        for g, (a, b) in enumerate(GATHER_GROUPS):
-            group_of[a] = g
-
-        def gather_for(e):
-            if e in group_of:
-                gather(group_of[e])
-
-        STAGES = (gather_for, first_a, first_b_and_activate, multiply, turn, turn_out, quantise, second_layer, results)
+        STAGES = (gather, first_layer, activate, multiply, turn, turn_out, quantise, second_layer, results)
         for step in range(E + len(STAGES) - 1):
             for lag in reversed(range(len(STAGES))):
                 if 0 <= step - lag < E:
                     STAGES[lag](step - lag)
 
-        BLOCKS = T // P
+        for a, tag in ((0, "pa"), (4, "pa"), (8, "pb")):
+            late = bank(tag, [P, 4 * C])
+            for x in range(a, a + 4):
+                second(x, 1, late[:, (x - a) * C : (x - a + 1) * C])
+            nc.scalar.copy(out=y[1][:, a * C : (a + 4) * C], in_=late[:])
 
         def fetch(r, half):
             nc.vector.tensor_tensor(prod[half][r][:], y[half][:].indirect(pos_t[r][:]), gate_t[:, r, :], MULT)
 
         turned_sum = {}
         partial = {}
-        TAGS = (("pa", "pa", "pb", "pb"), ("pt", "pt", "py", "py"))
+        TAGS = (("pt", "pt", "py", "pb"), ("pa", "pa", "pb", "pb"))
 
         def add_turned(r, half):
             for b in range(BLOCKS):
                 if r == 0:
-                    turned_sum[half, b] = psum.tile([P, P], F32, name=TAGS[half][b])
+                    turned_sum[half, b] = bank(TAGS[half][b], [P, P])
                 nc.tensor.matmul(
                     turned_sum[half, b][:],
                     lhsT=prod[half][r][:, b * P : (b + 1) * P],
@@ -266,7 +264,7 @@ def tile_moe_tk_glu_gelu_kernel(
                 )
 
         def turn_back(half):
-            partial[half] = psum.tile([P, T], F32, name=TAGS[half][3])
+            partial[half] = bank(TAGS[half][3], [P, T])
             for b in range(BLOCKS):
                 staged = keep.tile([P, P], F32, name=f"staged{half}{b}", align_bytes=64)
                 nc.scalar.copy(out=staged[:], in_=turned_sum[half, b][:])

@@ -26,9 +26,8 @@ ADD, MULT = mybir.AluOpType.add, mybir.AluOpType.mult
 
 GATHER_GROUPS = [(0, 1), (1, 3), (3, 5), (5, 7), (7, 9), (9, 11), (11, 12)]
 TURN_GROUPS = [(0, 1), (1, 3), (3, 5), (5, 7), (7, 9), (9, 11), (11, 12)]
-RESULT_GROUPS = [(0, 3), (3, 7), (7, 11), (11, 12)]
+RESULT_GROUPS = [(0, 3), (3, 7), (7, 9), (9, 12)]
 X_CHUNKS = [(0, 256, 160), (256, 384, 80)]
-BANKS = {"pa": 2, "pb": 3, "pt": 2, "py": 1}
 
 
 def tile_moe_tk_glu_gelu_kernel(
@@ -42,8 +41,19 @@ def tile_moe_tk_glu_gelu_kernel(
         slots = ctx.enter_context(tc.tile_pool(name="slots", bufs=2))
         psum = ctx.enter_context(tc.psum_pool(name="psum", bufs=1))
 
-        def bank(tag, shape):
-            return psum.tile(shape, F32, name=tag, bufs=BANKS[tag])
+        def bank(n, shape):
+            return psum.tile(shape, F32, name=f"bank{n}")
+
+        def bank_a(e):
+            return (0, 5)[e // 2 % 2] if e % 2 else 1
+
+        def bank_b(e):
+            return (2, 3, 4, 6)[e % 4]
+
+        def bank_turn(e):
+            return bank_a(e + 1) if e + 1 < E else bank_a(e - 1)
+
+        BANK_Y = 7
 
         offs_t = lists.tile([P, S // 16], U16, name="offs_t")
         pos_t = [lists.tile([P, T // 16], U16, name=f"pos_t{r}") for r in range(TOP)]
@@ -53,7 +63,7 @@ def tile_moe_tk_glu_gelu_kernel(
         cscale = keep.tile([P, WINDOW], U8, name="cscale", align_bytes=64)
         ident = keep.tile([P, P], F32, name="ident", align_bytes=64)
         warm = keep.tile([P, 1], F32, name="warm")
-        y = [keep.tile([P, S], F32, name=f"y{h}", align_bytes=64) for h in range(HALVES)]
+        y = [keep.tile([P, S], F32, name="y0", align_bytes=64)]
         prod = [[keep.tile([P, T], F32, name=f"prod{h}{r}", align_bytes=64) for r in range(TOP)] for h in range(HALVES)]
 
         nc.vector.memset(warm[:], 0.0)
@@ -92,23 +102,21 @@ def tile_moe_tk_glu_gelu_kernel(
             raw.append(chunk)
         nc.sync.dma_start(offs_t[:], offs)
         load_words(w1, "w1", w1_words, 0, 1)
-        load_scales(s1, "s1", w1_scales, 0, 4)
+        load_scales(s1, "s1", w1_scales, 0, 6)
         load_words(w3, "w3", w3_words, 0, 1)
-        load_scales(s3, "s3", w3_scales, 0, 4)
+        load_scales(s3, "s3", w3_scales, 0, 6)
         load_words(w1, "w1", w1_words, 1, 3)
         load_words(w3, "w3", w3_words, 1, 3)
-        load_words(w1, "w1", w1_words, 3, 5)
-        load_words(w3, "w3", w3_words, 3, 5)
-        load_scales(s1, "s1", w1_scales, 4, 12)
-        load_scales(s3, "s3", w3_scales, 4, 12)
-        load_words(w1, "w1", w1_words, 5, 8)
-        load_words(w3, "w3", w3_words, 5, 8)
+        load_words(w1, "w1", w1_words, 3, 6)
+        load_words(w3, "w3", w3_words, 3, 6)
+        load_scales(s1, "s1", w1_scales, 6, 12)
+        load_scales(s3, "s3", w3_scales, 6, 12)
+        load_words(w1, "w1", w1_words, 6, 9)
+        load_words(w3, "w3", w3_words, 6, 9)
         load_scales(s2, "s2", w2_scales, 0, 12)
         load_words(w2, "w2", w2_words, 0, 6)
-        load_words(w1, "w1", w1_words, 8, 10)
-        load_words(w3, "w3", w3_words, 8, 10)
-        load_words(w1, "w1", w1_words, 10, 12)
-        load_words(w3, "w3", w3_words, 10, 12)
+        load_words(w1, "w1", w1_words, 9, 12)
+        load_words(w3, "w3", w3_words, 9, 12)
         load_words(w2, "w2", w2_words, 6, 12)
         for r, pos in enumerate((pos1, pos2, pos3, pos4)):
             nc.sync.dma_start(pos_t[r][:], pos)
@@ -157,9 +165,9 @@ def tile_moe_tk_glu_gelu_kernel(
             )
 
         def first_layer(e):
-            pa[e] = bank("pa", [P, H])
+            pa[e] = bank(bank_a(e), [P, H])
             first(e, pa[e], w1, s1)
-            pb[e] = bank("pb", [P, H])
+            pb[e] = bank(bank_b(e), [P, H])
             first(e, pb[e], w3, s3)
 
         def activate(e):
@@ -181,7 +189,7 @@ def tile_moe_tk_glu_gelu_kernel(
 
         def turn(e):
             for a, b in ending(TURN_GROUPS, e):
-                pt = bank("pt", [P, b - a, 2, C])
+                pt = bank(bank_turn(e), [P, b - a, 2, C])
                 for x in range(a, b):
                     words = hidden[x][:].bitcast(F32)
                     for u in range(2):
@@ -190,7 +198,10 @@ def tile_moe_tk_glu_gelu_kernel(
 
         def turn_out(e):
             for a, b in ending(TURN_GROUPS, e):
-                ht = ring.tile([P, (b - a) * 4 * C], BF16, name="ht", align_bytes=64)
+                if b == E:
+                    ht = keep.tile([P, (b - a) * 4 * C], BF16, name="y1", align_bytes=64)
+                else:
+                    ht = ring.tile([P, (b - a) * 4 * C], BF16, name="ht", align_bytes=64)
                 nc.scalar.copy(
                     out=ht[:].bitcast(F32).rearrange("p (x s u) -> p x s u", x=b - a, u=2),
                     in_=turned_words[e][:].rearrange("p x u s -> p x s u"),
@@ -223,13 +234,16 @@ def tile_moe_tk_glu_gelu_kernel(
                 for x in range(first_x, end_x):
                     for a, b in RESULT_GROUPS:
                         if x == a:
-                            py[a] = bank("pb" if a == E - 1 else "py", [P, (b - a) * C])
+                            py[a] = bank(bank_a(E - 3) if b == E else BANK_Y, [P, (b - a) * C])
                         if a <= x < b:
                             second(x, 0, py[a][:, (x - a) * C : (x - a + 1) * C])
 
         def results(e):
             for a, b in ending(RESULT_GROUPS, e):
-                nc.scalar.copy(out=y[0][:, a * C : b * C], in_=py[a][:])
+                if b == E:
+                    nc.vector.tensor_copy(out=y[0][:, a * C : b * C], in_=py[a][:])
+                else:
+                    nc.scalar.copy(out=y[0][:, a * C : b * C], in_=py[a][:])
 
         STAGES = (gather, first_layer, activate, multiply, turn, turn_out, quantise, second_layer, results)
         for step in range(E + len(STAGES) - 1):
@@ -237,7 +251,8 @@ def tile_moe_tk_glu_gelu_kernel(
                 if 0 <= step - lag < E:
                     STAGES[lag](step - lag)
 
-        for a, tag in ((0, "pa"), (4, "pa"), (8, "pb")):
+        y.append(keep.tile([P, S], F32, name="y1", align_bytes=64))
+        for a, tag in ((4, bank_turn(E - 2)), (0, bank_turn(E - 1)), (8, bank_b(E - 1))):
             late = bank(tag, [P, 4 * C])
             for x in range(a, a + 4):
                 second(x, 1, late[:, (x - a) * C : (x - a + 1) * C])
@@ -248,7 +263,7 @@ def tile_moe_tk_glu_gelu_kernel(
 
         turned_sum = {}
         partial = {}
-        TAGS = (("pt", "pt", "py", "pb"), ("pa", "pa", "pb", "pb"))
+        TAGS = ((2, 3, 4, 7), (0, 1, 5, 6))
 
         def add_turned(r, half):
             for b in range(BLOCKS):

@@ -26,7 +26,7 @@ ADD, MULT = mybir.AluOpType.add, mybir.AluOpType.mult
 
 GATHER_GROUPS = [(0, 1), (1, 3), (3, 5), (5, 7), (7, 9), (9, 11), (11, 12)]
 TURN_GROUPS = [(0, 1), (1, 3), (3, 5), (5, 7), (7, 9), (9, 11), (11, 12)]
-RESULT_GROUPS = [(0, 3), (3, 7), (7, 9), (9, 12)]
+RESULT_GROUPS = [(0, 3), (3, 7), (7, 9), (9, 11), (11, 12)]
 X_CHUNKS = [(0, 256, 160), (256, 384, 80)]
 
 
@@ -44,16 +44,22 @@ def tile_moe_tk_glu_gelu_kernel(
         def bank(n, shape):
             return psum.tile(shape, F32, name=f"bank{n}")
 
+        FIRST, SECOND, W3 = (0, 5), (1, 7), (2, 3, 4, 6)
+
+        def group(e):
+            return (e + 1) // 2
+
         def bank_a(e):
-            return (0, 5)[e // 2 % 2] if e % 2 else 1
+            return (FIRST if e % 2 else SECOND)[group(e) % 2]
 
         def bank_b(e):
-            return (2, 3, 4, 6)[e % 4]
+            return W3[e % 4]
 
         def bank_turn(e):
-            return bank_a(e + 1) if e + 1 < E else bank_a(e - 1)
+            return SECOND[(group(e) + 1) % 2]
 
-        BANK_Y = 7
+        def bank_y(e):
+            return {0: FIRST[0], 3: FIRST[1], 7: FIRST[0], 9: bank_b(8), 11: bank_b(9)}[e]
 
         offs_t = lists.tile([P, S // 16], U16, name="offs_t")
         pos_t = [lists.tile([P, T // 16], U16, name=f"pos_t{r}") for r in range(TOP)]
@@ -102,22 +108,24 @@ def tile_moe_tk_glu_gelu_kernel(
             raw.append(chunk)
         nc.sync.dma_start(offs_t[:], offs)
         load_words(w1, "w1", w1_words, 0, 1)
-        load_scales(s1, "s1", w1_scales, 0, 6)
+        load_scales(s1, "s1", w1_scales, 0, 5)
         load_words(w3, "w3", w3_words, 0, 1)
-        load_scales(s3, "s3", w3_scales, 0, 6)
+        load_scales(s3, "s3", w3_scales, 0, 5)
         load_words(w1, "w1", w1_words, 1, 3)
         load_words(w3, "w3", w3_words, 1, 3)
-        load_words(w1, "w1", w1_words, 3, 6)
-        load_words(w3, "w3", w3_words, 3, 6)
-        load_scales(s1, "s1", w1_scales, 6, 12)
-        load_scales(s3, "s3", w3_scales, 6, 12)
-        load_words(w1, "w1", w1_words, 6, 9)
-        load_words(w3, "w3", w3_words, 6, 9)
+        load_words(w1, "w1", w1_words, 3, 5)
+        load_words(w3, "w3", w3_words, 3, 5)
+        load_scales(s1, "s1", w1_scales, 5, 12)
+        load_scales(s3, "s3", w3_scales, 5, 12)
+        load_words(w1, "w1", w1_words, 5, 7)
+        load_words(w3, "w3", w3_words, 5, 7)
+        load_words(w1, "w1", w1_words, 7, 9)
+        load_words(w3, "w3", w3_words, 7, 9)
         load_scales(s2, "s2", w2_scales, 0, 12)
-        load_words(w2, "w2", w2_words, 0, 6)
+        load_words(w2, "w2", w2_words, 0, 3)
         load_words(w1, "w1", w1_words, 9, 12)
         load_words(w3, "w3", w3_words, 9, 12)
-        load_words(w2, "w2", w2_words, 6, 12)
+        load_words(w2, "w2", w2_words, 3, 12)
         for r, pos in enumerate((pos1, pos2, pos3, pos4)):
             nc.sync.dma_start(pos_t[r][:], pos)
         nc.sync.dma_start(out=gate_t[:], in_=gate[:, 0:P, :].rearrange("r p t -> p r t"))
@@ -230,29 +238,36 @@ def tile_moe_tk_glu_gelu_kernel(
             )
 
         def second_layer(e):
-            for first_x, end_x in ending(TURN_GROUPS, e):
-                for x in range(first_x, end_x):
-                    for a, b in RESULT_GROUPS:
-                        if x == a:
-                            py[a] = bank(bank_a(E - 3) if b == E else BANK_Y, [P, (b - a) * C])
-                        if a <= x < b:
-                            second(x, 0, py[a][:, (x - a) * C : (x - a + 1) * C])
+            for a, b in ending(RESULT_GROUPS, e):
+                py[a] = bank(bank_y(a), [P, (b - a) * C])
+                for x in range(a, b):
+                    second(x, 0, py[a][:, (x - a) * C : (x - a + 1) * C])
 
         def results(e):
             for a, b in ending(RESULT_GROUPS, e):
-                if b == E:
+                if b >= E - 3:
                     nc.vector.tensor_copy(out=y[0][:, a * C : b * C], in_=py[a][:])
                 else:
                     nc.scalar.copy(out=y[0][:, a * C : b * C], in_=py[a][:])
 
-        STAGES = (gather, first_layer, activate, multiply, turn, turn_out, quantise, second_layer, results)
-        for step in range(E + len(STAGES) - 1):
-            for lag in reversed(range(len(STAGES))):
+        STAGES = (
+            (second_layer, 8),
+            (results, 8),
+            (quantise, 7),
+            (turn_out, 6),
+            (turn, 5),
+            (multiply, 3),
+            (activate, 2),
+            (first_layer, 1),
+            (gather, 0),
+        )
+        for step in range(E + STAGES[0][1]):
+            for stage, lag in STAGES:
                 if 0 <= step - lag < E:
-                    STAGES[lag](step - lag)
+                    stage(step - lag)
 
         y.append(keep.tile([P, S], F32, name="y1", align_bytes=64))
-        for a, tag in ((4, bank_turn(E - 2)), (0, bank_turn(E - 1)), (8, bank_b(E - 1))):
+        for a, tag in ((4, bank_turn(E - 2)), (0, bank_turn(E - 1)), (8, FIRST[1])):
             late = bank(tag, [P, 4 * C])
             for x in range(a, a + 4):
                 second(x, 1, late[:, (x - a) * C : (x - a + 1) * C])
@@ -263,7 +278,7 @@ def tile_moe_tk_glu_gelu_kernel(
 
         turned_sum = {}
         partial = {}
-        TAGS = ((2, 3, 4, 7), (0, 1, 5, 6))
+        TAGS = ((4, 6, 0, 2), (1, 7, 5, 3))
 
         def add_turned(r, half):
             for b in range(BLOCKS):
@@ -294,5 +309,6 @@ def tile_moe_tk_glu_gelu_kernel(
             fetch(TOP - 1, half)
         for half in range(HALVES):
             total = keep.tile([P, T], F32, name=f"total{half}", align_bytes=64)
-            nc.vector.tensor_tensor(total[:], partial[half][:], prod[half][TOP - 1][:], ADD)
-            nc.sync.dma_start(out=out[half * P : (half + 1) * P, :], in_=total[:])
+            for a, b in ((0, T),) if half == 0 else ((0, 2 * P), (2 * P, T)):
+                nc.vector.tensor_tensor(total[:, a:b], partial[half][:, a:b], prod[half][TOP - 1][:, a:b], ADD)
+                nc.sync.dma_start(out=out[half * P : (half + 1) * P, a:b], in_=total[:, a:b])

@@ -37,7 +37,7 @@ def tile_moe_tk_glu_gelu_kernel(
     with ExitStack() as ctx:
         lists = ctx.enter_context(tc.tile_pool(name="lists", bufs=1))
         keep = ctx.enter_context(tc.tile_pool(name="keep", bufs=1))
-        ring = ctx.enter_context(tc.tile_pool(name="ring", bufs=4))
+        ring = ctx.enter_context(tc.tile_pool(name="ring", bufs=12))
         slots = ctx.enter_context(tc.tile_pool(name="slots", bufs=2))
         psum = ctx.enter_context(tc.psum_pool(name="psum", bufs=1))
 
@@ -68,16 +68,12 @@ def tile_moe_tk_glu_gelu_kernel(
         codes = keep.tile([P, WINDOW], I32, name="codes", align_bytes=64)
         cscale = keep.tile([P, WINDOW], U8, name="cscale", align_bytes=64)
         ident = keep.tile([P, P], F32, name="ident", align_bytes=64)
-        warm = keep.tile([P, 1], F32, name="warm")
-        y = [keep.tile([P, S], F32, name="y0", align_bytes=64)]
+        y = [keep.tile([P, S], F32, name=f"y{h}", align_bytes=64) for h in range(HALVES)]
         prod = [[keep.tile([P, T], F32, name=f"prod{h}{r}", align_bytes=64) for r in range(TOP)] for h in range(HALVES)]
 
-        nc.vector.memset(warm[:], 0.0)
         nc.vector.memset(codes[:, T:WINDOW], 0)
         nc.gpsimd.memset(cscale[:], 0)
         make_identity(nc, ident[:])
-        warm_out = keep.tile([P, 1], F32, name="warm_out")
-        nc.scalar.activation(warm_out[:], warm[:], GELU)
 
         w1, w3, w2, s1, s3, s2 = {}, {}, {}, {}, {}, {}
 
@@ -111,20 +107,20 @@ def tile_moe_tk_glu_gelu_kernel(
         load_scales(s1, "s1", w1_scales, 0, 5)
         load_words(w3, "w3", w3_words, 0, 1)
         load_scales(s3, "s3", w3_scales, 0, 5)
-        load_words(w1, "w1", w1_words, 1, 3)
         load_words(w3, "w3", w3_words, 1, 3)
-        load_words(w1, "w1", w1_words, 3, 5)
+        load_words(w1, "w1", w1_words, 1, 3)
         load_words(w3, "w3", w3_words, 3, 5)
-        load_scales(s1, "s1", w1_scales, 5, 12)
+        load_words(w1, "w1", w1_words, 3, 5)
         load_scales(s3, "s3", w3_scales, 5, 12)
-        load_words(w1, "w1", w1_words, 5, 7)
+        load_scales(s1, "s1", w1_scales, 5, 12)
         load_words(w3, "w3", w3_words, 5, 7)
-        load_words(w1, "w1", w1_words, 7, 9)
+        load_words(w1, "w1", w1_words, 5, 7)
         load_words(w3, "w3", w3_words, 7, 9)
+        load_words(w1, "w1", w1_words, 7, 9)
         load_scales(s2, "s2", w2_scales, 0, 12)
         load_words(w2, "w2", w2_words, 0, 3)
-        load_words(w1, "w1", w1_words, 9, 12)
         load_words(w3, "w3", w3_words, 9, 12)
+        load_words(w1, "w1", w1_words, 9, 12)
         load_words(w2, "w2", w2_words, 3, 12)
         for r, pos in enumerate((pos1, pos2, pos3, pos4)):
             nc.sync.dma_start(pos_t[r][:], pos)
@@ -174,9 +170,10 @@ def tile_moe_tk_glu_gelu_kernel(
 
         def first_layer(e):
             pa[e] = bank(bank_a(e), [P, H])
-            first(e, pa[e], w1, s1)
             pb[e] = bank(bank_b(e), [P, H])
-            first(e, pb[e], w3, s3)
+            products = [(pb[e], w3, s3), (pa[e], w1, s1)]
+            for to, words, scales in reversed(products) if e == 0 else products:
+                first(e, to, words, scales)
 
         def activate(e):
             gelu[e] = ring.tile([P, H], F32, name="g", align_bytes=64)
@@ -206,10 +203,7 @@ def tile_moe_tk_glu_gelu_kernel(
 
         def turn_out(e):
             for a, b in ending(TURN_GROUPS, e):
-                if b == E:
-                    ht = keep.tile([P, (b - a) * 4 * C], BF16, name="y1", align_bytes=64)
-                else:
-                    ht = ring.tile([P, (b - a) * 4 * C], BF16, name="ht", align_bytes=64)
+                ht = ring.tile([P, (b - a) * 4 * C], BF16, name="ht", align_bytes=64)
                 nc.scalar.copy(
                     out=ht[:].bitcast(F32).rearrange("p (x s u) -> p x s u", x=b - a, u=2),
                     in_=turned_words[e][:].rearrange("p x u s -> p x s u"),
@@ -266,8 +260,7 @@ def tile_moe_tk_glu_gelu_kernel(
                 if 0 <= step - lag < E:
                     stage(step - lag)
 
-        y.append(keep.tile([P, S], F32, name="y1", align_bytes=64))
-        for a, tag in ((4, bank_turn(E - 2)), (0, bank_turn(E - 1)), (8, FIRST[1])):
+        for a, tag in ((8, bank_y(7)), (0, bank_y(9)), (4, bank_y(11))):
             late = bank(tag, [P, 4 * C])
             for x in range(a, a + 4):
                 second(x, 1, late[:, (x - a) * C : (x - a + 1) * C])
@@ -278,7 +271,7 @@ def tile_moe_tk_glu_gelu_kernel(
 
         turned_sum = {}
         partial = {}
-        TAGS = ((4, 6, 0, 2), (1, 7, 5, 3))
+        TAGS = ((1, 7, 5, 4), (0, 2, 3, 6))
 
         def add_turned(r, half):
             for b in range(BLOCKS):

@@ -9,6 +9,8 @@ S = E * C
 P = 128
 HALVES = N // P
 BLOCKS = T // P
+PACK = 4
+PER_COLUMN = 16
 WINDOW = 512
 
 FLOPS = 2 * S * (2 * K * H + H * N)
@@ -24,10 +26,17 @@ FP4X4 = mybir.dt.float4_e2m1fn_x4
 GELU = mybir.ActivationFunctionType.Gelu_apprx_tanh
 ADD, MULT = mybir.AluOpType.add, mybir.AluOpType.mult
 
-GATHER_GROUPS = [(0, 1), (1, 3), (3, 5), (5, 7), (7, 9), (9, 11), (11, 12)]
-TURN_GROUPS = [(0, 1), (1, 3), (3, 5), (5, 7), (7, 9), (9, 11), (11, 12)]
-RESULT_GROUPS = [(0, 3), (3, 7), (7, 9), (9, 11), (11, 12)]
-X_CHUNKS = [(0, 256, 160), (256, 384, 80)]
+X_LOADS = [(0, 256, 160), (256, T, 80)]
+
+GROUPS = [(0, 1)] + [(e, e + 2) for e in range(1, E - 1, 2)] + [(E - 1, E)]
+GATHERED_GROUPS = 3
+
+RESULT_RUNS = [(0, 3), (3, 7), (7, 9), (9, 11), (11, E)]
+RUNS_ON_SCALAR = 2
+LATE_RUN = 4
+
+EARLY_SCALES = 5
+LAST_WORDS = 9
 
 
 def tile_moe_tk_glu_gelu_kernel(
@@ -37,14 +46,13 @@ def tile_moe_tk_glu_gelu_kernel(
     with ExitStack() as ctx:
         lists = ctx.enter_context(tc.tile_pool(name="lists", bufs=1))
         keep = ctx.enter_context(tc.tile_pool(name="keep", bufs=1))
-        ring = ctx.enter_context(tc.tile_pool(name="ring", bufs=12))
-        slots = ctx.enter_context(tc.tile_pool(name="slots", bufs=2))
+        slots = ctx.enter_context(tc.tile_pool(name="slots", bufs=GATHERED_GROUPS))
         psum = ctx.enter_context(tc.psum_pool(name="psum", bufs=1))
 
-        def bank(n, shape):
-            return psum.tile(shape, F32, name=f"bank{n}")
-
         FIRST, SECOND, W3 = (0, 5), (1, 7), (2, 3, 4, 6)
+
+        def bank(number, shape):
+            return psum.tile(shape, F32, name=f"bank{number}")
 
         def group(e):
             return (e + 1) // 2
@@ -53,113 +61,117 @@ def tile_moe_tk_glu_gelu_kernel(
             return (FIRST if e % 2 else SECOND)[group(e) % 2]
 
         def bank_b(e):
-            return W3[e % 4]
+            return W3[e % len(W3)]
 
-        def bank_turn(e):
+        def bank_turned(e):
             return SECOND[(group(e) + 1) % 2]
 
-        def bank_y(e):
-            return {0: FIRST[0], 3: FIRST[1], 7: FIRST[0], 9: bank_b(8), 11: bank_b(9)}[e]
+        result_bank = [bank_a(7), bank_a(9), bank_a(11), bank_b(8), bank_b(9)]
 
-        offs_t = lists.tile([P, S // 16], U16, name="offs_t")
-        pos_t = [lists.tile([P, T // 16], U16, name=f"pos_t{r}") for r in range(TOP)]
+        offs_t = lists.tile([P, S // PER_COLUMN], U16, name="offs_t")
+        pos_t = [lists.tile([P, T // PER_COLUMN], U16, name=f"pos_t{r}") for r in range(TOP)]
 
         gate_t = keep.tile([P, TOP, T], F32, name="gate_t", align_bytes=64)
-        codes = keep.tile([P, WINDOW], I32, name="codes", align_bytes=64)
-        cscale = keep.tile([P, WINDOW], U8, name="cscale", align_bytes=64)
+        token_words = keep.tile([P, WINDOW], I32, name="token_words", align_bytes=64)
+        token_scales = keep.tile([P, WINDOW], U8, name="token_scales", align_bytes=64)
         ident = keep.tile([P, P], F32, name="ident", align_bytes=64)
-        y = [keep.tile([P, S], F32, name=f"y{h}", align_bytes=64) for h in range(HALVES)]
-        prod = [[keep.tile([P, T], F32, name=f"prod{h}{r}", align_bytes=64) for r in range(TOP)] for h in range(HALVES)]
+        y = [keep.tile([P, S], F32, name=f"y{half}", align_bytes=64) for half in range(HALVES)]
+        weighted = [
+            [keep.tile([P, T], F32, name=f"weighted{half}{r}", align_bytes=64) for r in range(TOP)]
+            for half in range(HALVES)
+        ]
 
-        nc.vector.memset(codes[:, T:WINDOW], 0)
-        nc.gpsimd.memset(cscale[:], 0)
+        nc.vector.memset(token_words[:, T:WINDOW], 0)
+        nc.gpsimd.memset(token_scales[:], 0)
         make_identity(nc, ident[:])
 
         w1, w3, w2, s1, s3, s2 = {}, {}, {}, {}, {}, {}
 
-        def load_words(held, tag, words, a, b):
-            tile = keep.tile([P, b - a, words.shape[3]], U8, name=f"{tag}_{a}", align_bytes=64)
+        def load_words(held, tag, words, first, end):
+            tile = keep.tile([P, end - first, words.shape[3]], U8, name=f"{tag}_{first}", align_bytes=64)
             nc.sync.dma_start(
                 out=tile[:].bitcast(I32),
-                in_=words[a:b, 0, :, :].rearrange("e p n -> p e n").bitcast(I32),
+                in_=words[first:end, 0, :, :].rearrange("e p n -> p e n").bitcast(I32),
             )
-            for e in range(a, b):
-                held[e] = tile[:, e - a, :]
+            for e in range(first, end):
+                held[e] = tile[:, e - first, :]
 
-        def load_scales(held, tag, scales, a, b):
-            tile = keep.tile([P, b - a, scales.shape[3]], U8, name=f"{tag}_{a}", align_bytes=64)
+        def load_scales(held, tag, scales, first, end):
+            tile = keep.tile([P, end - first, scales.shape[3]], U8, name=f"{tag}_{first}", align_bytes=64)
             for r in range(4):
                 nc.sync.dma_start(
                     out=tile[r:P:32, :, :].bitcast(I32),
-                    in_=scales[a:b, 0, r:16:4, :].rearrange("e q n -> q e n").bitcast(I32),
+                    in_=scales[first:end, 0, r:16:4, :].rearrange("e q n -> q e n").bitcast(I32),
                 )
-            for e in range(a, b):
-                held[e] = tile[:, e - a, :]
+            for e in range(first, end):
+                held[e] = tile[:, e - first, :]
 
-        x_rows = xT.rearrange("(p j) w -> p j w", j=4)
-        raw = []
-        for i, (a, b, split) in enumerate(X_CHUNKS):
-            chunk = keep.tile([P, 4, b - a], F32, name=f"raw{i}", align_bytes=64)
-            nc.sync.dma_start(out=chunk[:], in_=x_rows[:, :, a:b])
-            raw.append(chunk)
+        def load_first_layer_words(first, end):
+            load_words(w1, "w1", w1_words, first, end)
+            load_words(w3, "w3", w3_words, first, end)
+
+        x_rows = xT.rearrange("(p j) t -> p j t", j=PACK)
+        x_loaded = []
+        for first, end, on_vector in X_LOADS:
+            part = keep.tile([P, PACK, end - first], F32, name=f"x_{first}", align_bytes=64)
+            nc.sync.dma_start(out=part[:], in_=x_rows[:, :, first:end])
+            x_loaded.append(part)
         nc.sync.dma_start(offs_t[:], offs)
         load_words(w1, "w1", w1_words, 0, 1)
-        load_scales(s1, "s1", w1_scales, 0, 5)
+        load_scales(s1, "s1", w1_scales, 0, EARLY_SCALES)
         load_words(w3, "w3", w3_words, 0, 1)
-        load_scales(s3, "s3", w3_scales, 0, 5)
-        load_words(w3, "w3", w3_words, 1, 3)
-        load_words(w1, "w1", w1_words, 1, 3)
-        load_words(w3, "w3", w3_words, 3, 5)
-        load_words(w1, "w1", w1_words, 3, 5)
-        load_scales(s3, "s3", w3_scales, 5, 12)
-        load_scales(s1, "s1", w1_scales, 5, 12)
-        load_words(w3, "w3", w3_words, 5, 7)
-        load_words(w1, "w1", w1_words, 5, 7)
-        load_words(w3, "w3", w3_words, 7, 9)
-        load_words(w1, "w1", w1_words, 7, 9)
-        load_scales(s2, "s2", w2_scales, 0, 12)
-        load_words(w2, "w2", w2_words, 0, 3)
-        load_words(w3, "w3", w3_words, 9, 12)
-        load_words(w1, "w1", w1_words, 9, 12)
-        load_words(w2, "w2", w2_words, 3, 12)
+        load_scales(s3, "s3", w3_scales, 0, EARLY_SCALES)
+        for first, end in GROUPS[1:]:
+            if first == EARLY_SCALES:
+                load_scales(s1, "s1", w1_scales, EARLY_SCALES, E)
+                load_scales(s3, "s3", w3_scales, EARLY_SCALES, E)
+            if first < LAST_WORDS:
+                load_first_layer_words(first, end)
+        w2_cut = RESULT_RUNS[1][1]
+        load_scales(s2, "s2", w2_scales, 0, E)
+        load_words(w2, "w2", w2_words, 0, w2_cut)
+        load_first_layer_words(LAST_WORDS, E)
+        load_words(w2, "w2", w2_words, w2_cut, E)
         for r, pos in enumerate((pos1, pos2, pos3, pos4)):
             nc.sync.dma_start(pos_t[r][:], pos)
         nc.sync.dma_start(out=gate_t[:], in_=gate[:, 0:P, :].rearrange("r p t -> p r t"))
 
-        for i, (a, b, split) in enumerate(X_CHUNKS):
-            grouped = keep.tile([P, b - a, 4], BF16, name=f"grouped{i}", align_bytes=64)
-            turned = raw[i][:].rearrange("p j w -> p w j")
-            nc.vector.tensor_copy(out=grouped[:, :split, :], in_=turned[:, :split, :])
-            nc.scalar.copy(out=grouped[:, split:, :], in_=turned[:, split:, :])
+        for part, (first, end, on_vector) in zip(x_loaded, X_LOADS):
+            rounded = keep.tile([P, end - first, PACK], BF16, name=f"rounded_{first}", align_bytes=64)
+            by_token = part[:].rearrange("p j t -> p t j")
+            nc.vector.tensor_copy(out=rounded[:, :on_vector, :], in_=by_token[:, :on_vector, :])
+            nc.scalar.copy(out=rounded[:, on_vector:, :], in_=by_token[:, on_vector:, :])
             nc.vector.quantize_mx(
-                out=codes[:, a:b].bitcast(FP8X4),
-                scales=cscale[:, a:b],
-                in_=grouped[:].rearrange("p w j -> p (w j)"),
+                out=token_words[:, first:end].bitcast(FP8X4),
+                scales=token_scales[:, first:end],
+                in_=rounded[:].rearrange("p t j -> p (t j)"),
             )
 
-        slot_words, slot_scales, hidden_words, hidden_scales = {}, {}, {}, {}
-        pa, pb, gelu, hidden, turned_words, regrouped, py = {}, {}, {}, {}, {}, {}, {}
+        slot_words, slot_scales, h_words, h_scales = {}, {}, {}, {}
+        sums_a, sums_b, gelu_a, h, h_turned, h_packed, y_run = {}, {}, {}, {}, {}, {}, {}
 
-        def ending(groups, e):
-            return [(a, b) for a, b in groups if b - 1 == e]
+        def ending_at(spans, e):
+            return [(first, end) for first, end in spans if end - 1 == e]
+
+        def columns(e, first):
+            return slice((e - first) * C, (e - first + 1) * C)
 
         def gather(e):
-            for a, b in GATHER_GROUPS:
-                if a == e:
-                    width = (b - a) * C
-                    where = offs_t[:, a * C // 16 : b * C // 16]
-                    gs = slots.tile([P, width], U8, name="gs", align_bytes=64)
-                    nc.vector.tensor_copy(gs[:], cscale[:].indirect(where))
-                    gw = slots.tile([P, width], U32, name="gw", align_bytes=64)
-                    nc.vector.tensor_copy(gw[:], codes[:].bitcast(U32).indirect(where))
-                    for x in range(a, b):
-                        cols = slice((x - a) * C, (x - a + 1) * C)
-                        slot_words[x] = gw[:, cols]
-                        slot_scales[x] = gs[:, cols]
+            for first, end in GROUPS:
+                if first == e:
+                    width = (end - first) * C
+                    entries = offs_t[:, first * C // PER_COLUMN : end * C // PER_COLUMN]
+                    scales = slots.tile([P, width], U8, name="slot_scales", align_bytes=64)
+                    nc.vector.tensor_copy(scales[:], token_scales[:].indirect(entries))
+                    words = slots.tile([P, width], U32, name="slot_words", align_bytes=64)
+                    nc.vector.tensor_copy(words[:], token_words[:].bitcast(U32).indirect(entries))
+                    for member in range(first, end):
+                        slot_words[member] = words[:, columns(member, first)]
+                        slot_scales[member] = scales[:, columns(member, first)]
 
-        def first(e, to, words, scales):
+        def first_product(e, sums, words, scales):
             nc.tensor.matmul_mx(
-                out=to[:],
+                out=sums[:],
                 lhsT=slot_words[e].bitcast(FP8X4),
                 lhsT_scale=slot_scales[e],
                 rhs=words[e].bitcast(FP4X4),
@@ -169,117 +181,114 @@ def tile_moe_tk_glu_gelu_kernel(
             )
 
         def first_layer(e):
-            pa[e] = bank(bank_a(e), [P, H])
-            pb[e] = bank(bank_b(e), [P, H])
-            products = [(pb[e], w3, s3), (pa[e], w1, s1)]
-            for to, words, scales in reversed(products) if e == 0 else products:
-                first(e, to, words, scales)
+            sums_a[e] = bank(bank_a(e), [P, H])
+            first_product(e, sums_a[e], w1, s1)
+            sums_b[e] = bank(bank_b(e), [P, H])
+            first_product(e, sums_b[e], w3, s3)
+
+        def from_sums(sums):
+            return sums[:].rearrange("p (m u v) -> p u m v", u=2, v=2)
+
+        def by_pairs(tile):
+            return tile[:].rearrange("p (u m v) -> p u m v", u=2, v=2)
 
         def activate(e):
-            gelu[e] = ring.tile([P, H], F32, name="g", align_bytes=64)
-            nc.scalar.activation(
-                out=gelu[e][:].rearrange("p (u m v) -> p u m v", u=2, v=2),
-                in_=pa[e][:].rearrange("p (m u v) -> p u m v", u=2, v=2),
-                func=GELU,
-            )
+            gelu_a[e] = keep.tile([P, H], F32, name=f"gelu_a{e}", align_bytes=64)
+            nc.scalar.activation(out=by_pairs(gelu_a[e]), in_=from_sums(sums_a[e]), func=GELU)
 
         def multiply(e):
-            hidden[e] = ring.tile([P, H], BF16, name="h", align_bytes=64)
-            nc.vector.tensor_tensor(
-                out=hidden[e][:].rearrange("p (u m v) -> p u m v", u=2, v=2),
-                in0=pb[e][:].rearrange("p (m u v) -> p u m v", u=2, v=2),
-                in1=gelu[e][:].rearrange("p (u m v) -> p u m v", u=2, v=2),
-                op=MULT,
-            )
+            h[e] = keep.tile([P, H], BF16, name=f"h{e}", align_bytes=64)
+            nc.vector.tensor_tensor(out=by_pairs(h[e]), in0=from_sums(sums_b[e]), in1=by_pairs(gelu_a[e]), op=MULT)
 
         def turn(e):
-            for a, b in ending(TURN_GROUPS, e):
-                pt = bank(bank_turn(e), [P, b - a, 2, C])
-                for x in range(a, b):
-                    words = hidden[x][:].bitcast(F32)
+            for first, end in ending_at(GROUPS, e):
+                h_turned[e] = bank(bank_turned(e), [P, end - first, 2, C])
+                for member in range(first, end):
+                    pairs = h[member][:].bitcast(F32)
                     for u in range(2):
-                        nc.tensor.transpose(pt[:, x - a, u, :], words[:, u * P : (u + 1) * P], ident[:])
-                turned_words[e] = pt
+                        nc.tensor.transpose(
+                            h_turned[e][:, member - first, u, :], pairs[:, u * P : (u + 1) * P], ident[:]
+                        )
 
-        def turn_out(e):
-            for a, b in ending(TURN_GROUPS, e):
-                ht = ring.tile([P, (b - a) * 4 * C], BF16, name="ht", align_bytes=64)
+        def pack(e):
+            for first, end in ending_at(GROUPS, e):
+                h_packed[e] = keep.tile([P, (end - first) * C * PACK], BF16, name=f"h_packed{e}", align_bytes=64)
                 nc.scalar.copy(
-                    out=ht[:].bitcast(F32).rearrange("p (x s u) -> p x s u", x=b - a, u=2),
-                    in_=turned_words[e][:].rearrange("p x u s -> p x s u"),
+                    out=h_packed[e][:].bitcast(F32).rearrange("p (x s u) -> p x s u", x=end - first, u=2),
+                    in_=h_turned[e][:].rearrange("p x u s -> p x s u"),
                 )
-                regrouped[e] = ht
 
         def quantise(e):
-            for a, b in ending(TURN_GROUPS, e):
-                hw = keep.tile([P, (b - a) * C], U32, name=f"hw{a}", align_bytes=64)
-                hs = keep.tile([P, (b - a) * C], U8, name=f"hs{a}", align_bytes=64)
-                nc.vector.quantize_mx(out=hw[:].bitcast(FP8X4), scales=hs[:], in_=regrouped[e][:])
-                for x in range(a, b):
-                    cols = slice((x - a) * C, (x - a + 1) * C)
-                    hidden_words[x] = hw[:, cols]
-                    hidden_scales[x] = hs[:, cols]
+            for first, end in ending_at(GROUPS, e):
+                words = keep.tile([P, (end - first) * C], U32, name=f"h_words{first}", align_bytes=64)
+                scales = keep.tile([P, (end - first) * C], U8, name=f"h_scales{first}", align_bytes=64)
+                nc.vector.quantize_mx(out=words[:].bitcast(FP8X4), scales=scales[:], in_=h_packed[e][:])
+                for member in range(first, end):
+                    h_words[member] = words[:, columns(member, first)]
+                    h_scales[member] = scales[:, columns(member, first)]
 
-        def second(e, half, to):
+        def second_product(e, half, sums):
             nc.tensor.matmul_mx(
-                out=to,
+                out=sums,
                 lhsT=w2[e][:, 2 * P * half : 2 * P * (half + 1)].bitcast(FP4X4),
                 lhsT_scale=s2[e][:, P * half : P * (half + 1)],
-                rhs=hidden_words[e].bitcast(FP8X4),
-                rhs_scale=hidden_scales[e],
+                rhs=h_words[e].bitcast(FP8X4),
+                rhs_scale=h_scales[e],
                 start=True,
                 stop=True,
             )
 
         def second_layer(e):
-            for a, b in ending(RESULT_GROUPS, e):
-                py[a] = bank(bank_y(a), [P, (b - a) * C])
-                for x in range(a, b):
-                    second(x, 0, py[a][:, (x - a) * C : (x - a + 1) * C])
+            for first, end in ending_at(RESULT_RUNS, e):
+                y_run[first] = bank(result_bank[RESULT_RUNS.index((first, end))], [P, (end - first) * C])
+                for member in range(first, end):
+                    second_product(member, 0, y_run[first][:, columns(member, first)])
 
         def results(e):
-            for a, b in ending(RESULT_GROUPS, e):
-                if b >= E - 3:
-                    nc.vector.tensor_copy(out=y[0][:, a * C : b * C], in_=py[a][:])
+            for first, end in ending_at(RESULT_RUNS, e):
+                if RESULT_RUNS.index((first, end)) < RUNS_ON_SCALAR:
+                    nc.scalar.copy(out=y[0][:, first * C : end * C], in_=y_run[first][:])
                 else:
-                    nc.scalar.copy(out=y[0][:, a * C : b * C], in_=py[a][:])
+                    nc.vector.tensor_copy(out=y[0][:, first * C : end * C], in_=y_run[first][:])
 
-        STAGES = (
+        stages = (
             (second_layer, 8),
             (results, 8),
             (quantise, 7),
-            (turn_out, 6),
+            (pack, 6),
             (turn, 5),
             (multiply, 3),
             (activate, 2),
             (first_layer, 1),
             (gather, 0),
         )
-        for step in range(E + STAGES[0][1]):
-            for stage, lag in STAGES:
+        for step in range(E + stages[0][1]):
+            for stage, lag in stages:
                 if 0 <= step - lag < E:
                     stage(step - lag)
 
-        for a, tag in ((8, bank_y(7)), (0, bank_y(9)), (4, bank_y(11))):
-            late = bank(tag, [P, 4 * C])
-            for x in range(a, a + 4):
-                second(x, 1, late[:, (x - a) * C : (x - a + 1) * C])
-            nc.scalar.copy(out=y[1][:, a * C : (a + 4) * C], in_=late[:])
+        late_firsts = (E - LATE_RUN, 0, LATE_RUN)
+        late_banks = result_bank[-len(late_firsts) :]
+        for first, number in zip(late_firsts, late_banks):
+            late = bank(number, [P, LATE_RUN * C])
+            for member in range(first, first + LATE_RUN):
+                second_product(member, 1, late[:, columns(member, first)])
+            nc.scalar.copy(out=y[1][:, first * C : (first + LATE_RUN) * C], in_=late[:])
+
+        sum_banks = ([*SECOND, FIRST[1]], late_banks)
+        back_banks = (bank_b(E - 2), bank_b(E - 1))
+        turned_sum, three = {}, {}
 
         def fetch(r, half):
-            nc.vector.tensor_tensor(prod[half][r][:], y[half][:].indirect(pos_t[r][:]), gate_t[:, r, :], MULT)
-
-        turned_sum = {}
-        partial = {}
-        TAGS = ((1, 7, 5, 4), (0, 2, 3, 6))
+            nc.vector.tensor_tensor(weighted[half][r][:], y[half][:].indirect(pos_t[r][:]), gate_t[:, r, :], MULT)
 
         def add_turned(r, half):
             for b in range(BLOCKS):
                 if r == 0:
-                    turned_sum[half, b] = bank(TAGS[half][b], [P, P])
+                    turned_sum[half, b] = bank(sum_banks[half][b], [P, P])
                 nc.tensor.matmul(
                     turned_sum[half, b][:],
-                    lhsT=prod[half][r][:, b * P : (b + 1) * P],
+                    lhsT=weighted[half][r][:, b * P : (b + 1) * P],
                     rhs=ident[:],
                     is_transpose=True,
                     start=(r == 0),
@@ -287,11 +296,11 @@ def tile_moe_tk_glu_gelu_kernel(
                 )
 
         def turn_back(half):
-            partial[half] = bank(TAGS[half][3], [P, T])
+            three[half] = bank(back_banks[half], [P, T])
             for b in range(BLOCKS):
                 staged = keep.tile([P, P], F32, name=f"staged{half}{b}", align_bytes=64)
                 nc.scalar.copy(out=staged[:], in_=turned_sum[half, b][:])
-                nc.tensor.transpose(partial[half][:, b * P : (b + 1) * P], staged[:], ident[:])
+                nc.tensor.transpose(three[half][:, b * P : (b + 1) * P], staged[:], ident[:])
 
         for half in range(HALVES):
             for r in range(TOP - 1):
@@ -300,8 +309,12 @@ def tile_moe_tk_glu_gelu_kernel(
             turn_back(half)
         for half in range(HALVES):
             fetch(TOP - 1, half)
+
+        pieces = ([(0, T)], [(0, T - P), (T - P, T)])
         for half in range(HALVES):
             total = keep.tile([P, T], F32, name=f"total{half}", align_bytes=64)
-            for a, b in ((0, T),) if half == 0 else ((0, 2 * P), (2 * P, T)):
-                nc.vector.tensor_tensor(total[:, a:b], partial[half][:, a:b], prod[half][TOP - 1][:, a:b], ADD)
-                nc.sync.dma_start(out=out[half * P : (half + 1) * P, a:b], in_=total[:, a:b])
+            for first, end in pieces[half]:
+                nc.vector.tensor_tensor(
+                    total[:, first:end], three[half][:, first:end], weighted[half][TOP - 1][:, first:end], ADD
+                )
+                nc.sync.dma_start(out=out[half * P : (half + 1) * P, first:end], in_=total[:, first:end])

@@ -28,15 +28,14 @@ ADD, MULT = mybir.AluOpType.add, mybir.AluOpType.mult
 
 X_LOADS = [(0, 256, 160), (256, T, 80)]
 
-GROUPS = [(0, 1)] + [(e, e + 2) for e in range(1, E - 1, 2)] + [(E - 1, E)]
-GATHERED_GROUPS = 3
-
-RESULT_RUNS = [(0, 3), (3, 7), (7, 9), (9, 11), (11, E)]
-RUNS_ON_SCALAR = 2
+GATHERS = [(0, 1), (1, 3), (3, 6), (6, 9), (9, E)]
+ON_GPSIMD = 2
+PAIRS = E // 2
+QUANTISED = [(2, 3), (0, 4), (1,), (5,)]
+PACKS_ON_VECTOR = (0,)
 LATE_RUN = 4
-
+WORD_LOADS = [(1, 3), (3, 5), (5, 7), (7, 9), (9, E)]
 EARLY_SCALES = 5
-LAST_WORDS = 9
 
 
 def tile_moe_tk_glu_gelu_kernel(
@@ -46,27 +45,21 @@ def tile_moe_tk_glu_gelu_kernel(
     with ExitStack() as ctx:
         lists = ctx.enter_context(tc.tile_pool(name="lists", bufs=1))
         keep = ctx.enter_context(tc.tile_pool(name="keep", bufs=1))
-        slots = ctx.enter_context(tc.tile_pool(name="slots", bufs=GATHERED_GROUPS))
         psum = ctx.enter_context(tc.psum_pool(name="psum", bufs=1))
 
-        FIRST, SECOND, W3 = (0, 5), (1, 7), (2, 3, 4, 6)
+        W1, W3 = (0, 1, 5, 7), (2, 3, 4, 6)
 
         def bank(number, shape):
             return psum.tile(shape, F32, name=f"bank{number}")
 
-        def group(e):
-            return (e + 1) // 2
-
         def bank_a(e):
-            return (FIRST if e % 2 else SECOND)[group(e) % 2]
+            return W1[e % len(W1)]
 
         def bank_b(e):
             return W3[e % len(W3)]
 
-        def bank_turned(e):
-            return SECOND[(group(e) + 1) % 2]
-
-        result_bank = [bank_a(7), bank_a(9), bank_a(11), bank_b(8), bank_b(9)]
+        turned_after = (10, 8, 8, 9, 11, 9)
+        result_bank = [bank_b(e) for e in range(E - 4, E)]
 
         offs_t = lists.tile([P, S // PER_COLUMN], U16, name="offs_t")
         pos_t = [lists.tile([P, T // PER_COLUMN], U16, name=f"pos_t{r}") for r in range(TOP)]
@@ -118,29 +111,34 @@ def tile_moe_tk_glu_gelu_kernel(
             x_loaded.append(part)
         nc.sync.dma_start(offs_t[:], offs)
         load_words(w1, "w1", w1_words, 0, 1)
-        load_scales(s1, "s1", w1_scales, 0, EARLY_SCALES)
+        load_scales(s1, "s1", w1_scales, 0, 5)
         load_words(w3, "w3", w3_words, 0, 1)
-        load_scales(s3, "s3", w3_scales, 0, EARLY_SCALES)
-        for first, end in GROUPS[1:]:
-            if first == EARLY_SCALES:
-                load_scales(s1, "s1", w1_scales, EARLY_SCALES, E)
-                load_scales(s3, "s3", w3_scales, EARLY_SCALES, E)
-            if first < LAST_WORDS:
-                load_first_layer_words(first, end)
-        w2_cut = RESULT_RUNS[1][1]
-        load_scales(s2, "s2", w2_scales, 0, E)
-        load_words(w2, "w2", w2_words, 0, w2_cut)
-        load_first_layer_words(LAST_WORDS, E)
-        load_words(w2, "w2", w2_words, w2_cut, E)
+        load_scales(s3, "s3", w3_scales, 0, 5)
+        load_words(w1, "w1", w1_words, 1, 3)
+        load_words(w3, "w3", w3_words, 1, 3)
+        load_words(w1, "w1", w1_words, 3, 5)
+        load_words(w3, "w3", w3_words, 3, 5)
+        load_scales(s1, "s1", w1_scales, 5, 12)
+        load_scales(s3, "s3", w3_scales, 5, 12)
+        load_words(w1, "w1", w1_words, 5, 7)
+        load_words(w3, "w3", w3_words, 5, 7)
+        load_words(w1, "w1", w1_words, 7, 9)
+        load_words(w3, "w3", w3_words, 7, 9)
+        load_words(w1, "w1", w1_words, 9, 12)
+        load_words(w3, "w3", w3_words, 9, 12)
+        load_scales(s2, "s2", w2_scales, 0, 12)
+        load_words(w2, "w2", w2_words, 0, 8)
+        load_words(w2, "w2", w2_words, 8, 12)
         for r, pos in enumerate((pos1, pos2, pos3, pos4)):
             nc.sync.dma_start(pos_t[r][:], pos)
         nc.sync.dma_start(out=gate_t[:], in_=gate[:, 0:P, :].rearrange("r p t -> p r t"))
 
         for part, (first, end, on_vector) in zip(x_loaded, X_LOADS):
             rounded = keep.tile([P, end - first, PACK], BF16, name=f"rounded_{first}", align_bytes=64)
-            by_token = part[:].rearrange("p j t -> p t j")
-            nc.vector.tensor_copy(out=rounded[:, :on_vector, :], in_=by_token[:, :on_vector, :])
-            nc.scalar.copy(out=rounded[:, on_vector:, :], in_=by_token[:, on_vector:, :])
+            source = part[:].rearrange("p j (c i) -> p c j i", i=4)
+            target = rounded[:].rearrange("p (c i) j -> p c j i", i=4)
+            nc.vector.tensor_copy(out=target[:, : on_vector // 4], in_=source[:, : on_vector // 4])
+            nc.scalar.copy(out=target[:, on_vector // 4 :], in_=source[:, on_vector // 4 :])
             nc.vector.quantize_mx(
                 out=token_words[:, first:end].bitcast(FP8X4),
                 scales=token_scales[:, first:end],
@@ -148,7 +146,7 @@ def tile_moe_tk_glu_gelu_kernel(
             )
 
         slot_words, slot_scales, h_words, h_scales = {}, {}, {}, {}
-        sums_a, sums_b, gelu_a, h, h_turned, h_packed, y_run = {}, {}, {}, {}, {}, {}, {}
+        sums_a, sums_b, gelu_a, staged_b, h, h_turned, h_packed, y_run = {}, {}, {}, {}, {}, {}, {}, {}
 
         def ending_at(spans, e):
             return [(first, end) for first, end in spans if end - 1 == e]
@@ -156,18 +154,16 @@ def tile_moe_tk_glu_gelu_kernel(
         def columns(e, first):
             return slice((e - first) * C, (e - first + 1) * C)
 
-        def gather(e):
-            for first, end in GROUPS:
-                if first == e:
-                    width = (end - first) * C
-                    entries = offs_t[:, first * C // PER_COLUMN : end * C // PER_COLUMN]
-                    scales = slots.tile([P, width], U8, name="slot_scales", align_bytes=64)
-                    nc.vector.tensor_copy(scales[:], token_scales[:].indirect(entries))
-                    words = slots.tile([P, width], U32, name="slot_words", align_bytes=64)
-                    nc.vector.tensor_copy(words[:], token_words[:].bitcast(U32).indirect(entries))
-                    for member in range(first, end):
-                        slot_words[member] = words[:, columns(member, first)]
-                        slot_scales[member] = scales[:, columns(member, first)]
+        for first, end in GATHERS:
+            width = (end - first) * C
+            entries = offs_t[:, first * C // PER_COLUMN : end * C // PER_COLUMN]
+            scales = keep.tile([P, width], U8, name=f"slot_scales{first}", align_bytes=64)
+            nc.vector.tensor_copy(scales[:], token_scales[:].indirect(entries))
+            words = keep.tile([P, width], U32, name=f"slot_words{first}", align_bytes=64)
+            nc.vector.tensor_copy(words[:], token_words[:].bitcast(U32).indirect(entries))
+            for member in range(first, end):
+                slot_words[member] = words[:, columns(member, first)]
+                slot_scales[member] = scales[:, columns(member, first)]
 
         def first_product(e, sums, words, scales):
             nc.tensor.matmul_mx(
@@ -196,36 +192,50 @@ def tile_moe_tk_glu_gelu_kernel(
             gelu_a[e] = keep.tile([P, H], F32, name=f"gelu_a{e}", align_bytes=64)
             nc.scalar.activation(out=by_pairs(gelu_a[e]), in_=from_sums(sums_a[e]), func=GELU)
 
+            if e < ON_GPSIMD:
+                staged_b[e] = keep.tile([P, H], F32, name=f"staged_b{e}", align_bytes=64)
+                nc.scalar.copy(out=by_pairs(staged_b[e]), in_=from_sums(sums_b[e]))
+
         def multiply(e):
-            h[e] = keep.tile([P, H], BF16, name=f"h{e}", align_bytes=64)
-            nc.vector.tensor_tensor(out=by_pairs(h[e]), in0=from_sums(sums_b[e]), in1=by_pairs(gelu_a[e]), op=MULT)
-
-        def turn(e):
-            for first, end in ending_at(GROUPS, e):
-                h_turned[e] = bank(bank_turned(e), [P, end - first, 2, C])
-                for member in range(first, end):
-                    pairs = h[member][:].bitcast(F32)
-                    for u in range(2):
-                        nc.tensor.transpose(
-                            h_turned[e][:, member - first, u, :], pairs[:, u * P : (u + 1) * P], ident[:]
-                        )
-
-        def pack(e):
-            for first, end in ending_at(GROUPS, e):
-                h_packed[e] = keep.tile([P, (end - first) * C * PACK], BF16, name=f"h_packed{e}", align_bytes=64)
-                nc.scalar.copy(
-                    out=h_packed[e][:].bitcast(F32).rearrange("p (x s u) -> p x s u", x=end - first, u=2),
-                    in_=h_turned[e][:].rearrange("p x u s -> p x s u"),
+            name = "token_words" if e == 0 else f"h{e}"
+            h[e] = keep.tile([P, H], BF16, name=name, align_bytes=64)
+            if e < ON_GPSIMD:
+                nc.gpsimd.tensor_tensor(out=h[e][:], in0=staged_b[e][:], in1=gelu_a[e][:], op=MULT)
+            else:
+                nc.vector.tensor_tensor(
+                    out=by_pairs(h[e]), in0=from_sums(sums_b[e]), in1=by_pairs(gelu_a[e]), op=MULT
                 )
 
-        def quantise(e):
-            for first, end in ending_at(GROUPS, e):
-                words = keep.tile([P, (end - first) * C], U32, name=f"h_words{first}", align_bytes=64)
-                scales = keep.tile([P, (end - first) * C], U8, name=f"h_scales{first}", align_bytes=64)
-                nc.vector.quantize_mx(out=words[:].bitcast(FP8X4), scales=scales[:], in_=h_packed[e][:])
-                for member in range(first, end):
-                    h_words[member] = words[:, columns(member, first)]
-                    h_scales[member] = scales[:, columns(member, first)]
+        def turn(j):
+            h_turned[j] = bank(bank_a(turned_after[j]), [P, 2, 2, C])
+            for member in range(2):
+                words = h[2 * j + member][:].bitcast(F32)
+                for u in range(2):
+                    nc.tensor.transpose(h_turned[j][:, member, u, :], words[:, u * P : (u + 1) * P], ident[:])
+
+        for group in QUANTISED:
+            tile = keep.tile([P, len(group) * 2 * C * PACK], BF16, name=f"h_packed{group[0]}", align_bytes=64)
+            h_packed[group] = tile
+            for place, j in enumerate(group):
+                h_packed[j] = tile[:, place * 2 * C * PACK : (place + 1) * 2 * C * PACK]
+
+        def pack(j):
+            (nc.vector.tensor_copy if j in PACKS_ON_VECTOR else nc.scalar.copy)(
+                out=h_packed[j].bitcast(F32).rearrange("p (x s u) -> p x s u", x=2, u=2),
+                in_=h_turned[j][:].rearrange("p x u s -> p x s u"),
+            )
+
+        def members(group):
+            return [2 * j + member for j in group for member in range(2)]
+
+        def quantise(group):
+            width = len(group) * 2 * C
+            words = keep.tile([P, width], U32, name=f"h_words{group[0]}", align_bytes=64)
+            scales = keep.tile([P, width], U8, name=f"h_scales{group[0]}", align_bytes=64)
+            nc.vector.quantize_mx(out=words[:].bitcast(FP8X4), scales=scales[:], in_=h_packed[group][:])
+            for place, e in enumerate(members(group)):
+                h_words[e] = words[:, columns(place, 0)]
+                h_scales[e] = scales[:, columns(place, 0)]
 
         def second_product(e, half, sums):
             nc.tensor.matmul_mx(
@@ -238,45 +248,38 @@ def tile_moe_tk_glu_gelu_kernel(
                 stop=True,
             )
 
-        def second_layer(e):
-            for first, end in ending_at(RESULT_RUNS, e):
-                y_run[first] = bank(result_bank[RESULT_RUNS.index((first, end))], [P, (end - first) * C])
-                for member in range(first, end):
-                    second_product(member, 0, y_run[first][:, columns(member, first)])
+        def second_layer(group):
+            y_run[group] = bank(result_bank[QUANTISED.index(group)], [P, len(group), 2 * C])
+            for place, e in enumerate(members(group)):
+                second_product(e, 0, y_run[group][:, place // 2, columns(place % 2, 0)])
 
-        def results(e):
-            for first, end in ending_at(RESULT_RUNS, e):
-                if RESULT_RUNS.index((first, end)) < RUNS_ON_SCALAR:
-                    nc.scalar.copy(out=y[0][:, first * C : end * C], in_=y_run[first][:])
-                else:
-                    nc.vector.tensor_copy(out=y[0][:, first * C : end * C], in_=y_run[first][:])
+        def results(group, copy):
+            by_pair = y[0][:].rearrange("p (j x) -> p j x", j=PAIRS)
+            copy(out=by_pair[:, group[0] : group[-1] + 1 : max(group[-1] - group[0], 1), :], in_=y_run[group][:])
 
-        stages = (
-            (second_layer, 8),
-            (results, 8),
-            (quantise, 7),
-            (pack, 6),
-            (turn, 5),
-            (multiply, 3),
-            (activate, 2),
-            (first_layer, 1),
-            (gather, 0),
-        )
-        for step in range(E + stages[0][1]):
-            for stage, lag in stages:
+        for step in range(E + 2):
+            for stage, lag in ((multiply, 2), (activate, 1), (first_layer, 0)):
                 if 0 <= step - lag < E:
                     stage(step - lag)
+        for j in (2, 3, 0, 4, 1, 5):
+            turn(j)
+            pack(j)
+        for group in QUANTISED:
+            quantise(group)
+            second_layer(group)
+        for group, copy in zip(QUANTISED, (nc.scalar.copy, nc.scalar.copy, nc.vector.tensor_copy, nc.vector.tensor_copy)):
+            results(group, copy)
 
         late_firsts = (E - LATE_RUN, 0, LATE_RUN)
-        late_banks = result_bank[-len(late_firsts) :]
+        late_banks = (result_bank[0], result_bank[1], result_bank[3])
         for first, number in zip(late_firsts, late_banks):
             late = bank(number, [P, LATE_RUN * C])
             for member in range(first, first + LATE_RUN):
                 second_product(member, 1, late[:, columns(member, first)])
             nc.scalar.copy(out=y[1][:, first * C : (first + LATE_RUN) * C], in_=late[:])
 
-        sum_banks = ([*SECOND, FIRST[1]], late_banks)
-        back_banks = (bank_b(E - 2), bank_b(E - 1))
+        sum_banks = ([bank_a(8), bank_a(10), bank_a(11)], late_banks)
+        back_banks = (bank_a(9), result_bank[2])
         turned_sum, three = {}, {}
 
         def fetch(r, half):

@@ -31,8 +31,8 @@ X_LOADS = [(0, 256, 160), (256, T, 80)]
 GATHERS = [(0, 1), (1, 3), (3, 6), (6, 9), (9, E)]
 ON_GPSIMD = 2
 PAIRS = E // 2
-QUANTISED = [(2, 3), (0, 4), (1,), (5,)]
-PACKS_ON_VECTOR = (0,)
+QUANTISED = [(0, 1), (2, 3), (4,), (5,)]
+PACKS_ON_VECTOR = ()
 LATE_RUN = 4
 WORD_LOADS = [(1, 3), (3, 5), (5, 7), (7, 9), (9, E)]
 EARLY_SCALES = 5
@@ -58,7 +58,7 @@ def tile_moe_tk_glu_gelu_kernel(
         def bank_b(e):
             return W3[e % len(W3)]
 
-        turned_after = (10, 8, 8, 9, 11, 9)
+        turned_after = (3, 5, 8, 9, 10, 11)
         result_bank = [bank_b(e) for e in range(E - 4, E)]
 
         offs_t = lists.tile([P, S // PER_COLUMN], U16, name="offs_t")
@@ -116,16 +116,17 @@ def tile_moe_tk_glu_gelu_kernel(
         load_scales(s3, "s3", w3_scales, 0, 5)
         load_words(w1, "w1", w1_words, 1, 3)
         load_words(w3, "w3", w3_words, 1, 3)
+        load_scales(s1, "s1", w1_scales, 5, 12)
         load_words(w1, "w1", w1_words, 3, 5)
         load_words(w3, "w3", w3_words, 3, 5)
-        load_scales(s1, "s1", w1_scales, 5, 12)
         load_scales(s3, "s3", w3_scales, 5, 12)
         load_words(w1, "w1", w1_words, 5, 7)
         load_words(w3, "w3", w3_words, 5, 7)
         load_words(w1, "w1", w1_words, 7, 9)
         load_words(w3, "w3", w3_words, 7, 9)
         load_words(w1, "w1", w1_words, 9, 12)
-        load_words(w3, "w3", w3_words, 9, 12)
+        load_words(w3, "w3", w3_words, 9, 11)
+        load_words(w3, "w3", w3_words, 11, 12)
         load_scales(s2, "s2", w2_scales, 0, 12)
         load_words(w2, "w2", w2_words, 0, 8)
         load_words(w2, "w2", w2_words, 8, 12)
@@ -197,7 +198,7 @@ def tile_moe_tk_glu_gelu_kernel(
                 nc.scalar.copy(out=by_pairs(staged_b[e]), in_=from_sums(sums_b[e]))
 
         def multiply(e):
-            name = "token_words" if e == 0 else f"h{e}"
+            name = "h0" if e == 0 else f"h{e}"
             h[e] = keep.tile([P, H], BF16, name=name, align_bytes=64)
             if e < ON_GPSIMD:
                 nc.gpsimd.tensor_tensor(out=h[e][:], in0=staged_b[e][:], in1=gelu_a[e][:], op=MULT)
@@ -258,10 +259,13 @@ def tile_moe_tk_glu_gelu_kernel(
             copy(out=by_pair[:, group[0] : group[-1] + 1 : max(group[-1] - group[0], 1), :], in_=y_run[group][:])
 
         for step in range(E + 2):
+            if step in {5: 0, 7: 1}:
+                turn({5: 0, 7: 1}[step])
+                pack({5: 0, 7: 1}[step])
             for stage, lag in ((multiply, 2), (activate, 1), (first_layer, 0)):
                 if 0 <= step - lag < E:
                     stage(step - lag)
-        for j in (2, 3, 0, 4, 1, 5):
+        for j in (2, 3, 4, 5):
             turn(j)
             pack(j)
         for group in QUANTISED:

@@ -29,10 +29,12 @@ ADD, MULT = mybir.AluOpType.add, mybir.AluOpType.mult
 X_LOADS = [(0, 256, 160), (256, T, 80)]
 
 GATHERS = [(0, 1), (1, 3), (3, 6), (6, 9), (9, E)]
-ON_GPSIMD = 2
-PAIRS = E // 2
-QUANTISED = [(0, 1), (2, 3), (4,), (5,)]
+ON_GPSIMD = 3
+TURNED = [(0, 2), (2, 4), (4, 6), (6, 8), (8, 10), (10, 11), (11, 12)]
+QUANTISED = [(0, 4), (4, 8), (8, 10), (10, 12)]
+RESULTS = [(0, 4), (4, 8), (8, 10), (10, 12)]
 PACKS_ON_VECTOR = ()
+SUMMED = ((0, 1, 2), (1, 2, 0))
 LATE_RUN = 4
 WORD_LOADS = [(1, 3), (3, 5), (5, 7), (7, 9), (9, E)]
 EARLY_SCALES = 5
@@ -58,19 +60,21 @@ def tile_moe_tk_glu_gelu_kernel(
         def bank_b(e):
             return W3[e % len(W3)]
 
-        turned_after = (3, 5, 8, 9, 10, 11)
+        turn_bank = (bank_a(3), bank_a(5), bank_a(8), bank_a(9), bank_a(10), bank_a(11), bank_a(8))
         result_bank = [bank_b(e) for e in range(E - 4, E)]
 
         offs_t = lists.tile([P, S // PER_COLUMN], U16, name="offs_t")
         pos_t = [lists.tile([P, T // PER_COLUMN], U16, name=f"pos_t{r}") for r in range(TOP)]
 
-        gate_t = keep.tile([P, TOP, T], F32, name="gate_t", align_bytes=64)
+        gate_first = keep.tile([P, T], F32, name="gate_first", align_bytes=64)
+        gate_rest = keep.tile([P, TOP - 1, T], F32, name="gate_rest", align_bytes=64)
+        gates = [gate_first[:]] + [gate_rest[:, r, :] for r in range(TOP - 1)]
         token_words = keep.tile([P, WINDOW], I32, name="token_words", align_bytes=64)
         token_scales = keep.tile([P, WINDOW], U8, name="token_scales", align_bytes=64)
         ident = keep.tile([P, P], F32, name="ident", align_bytes=64)
         y = [keep.tile([P, S], F32, name=f"y{half}", align_bytes=64) for half in range(HALVES)]
         weighted = [
-            [keep.tile([P, T], F32, name=f"weighted{half}{r}", align_bytes=64) for r in range(TOP)]
+            [keep.tile([P, T], F32, name="weighted01" if (half, r) == (1, 0) else f"weighted{half}{r}", align_bytes=64) for r in range(TOP)]
             for half in range(HALVES)
         ]
 
@@ -132,7 +136,9 @@ def tile_moe_tk_glu_gelu_kernel(
         load_words(w2, "w2", w2_words, 8, 12)
         for r, pos in enumerate((pos1, pos2, pos3, pos4)):
             nc.sync.dma_start(pos_t[r][:], pos)
-        nc.sync.dma_start(out=gate_t[:], in_=gate[:, 0:P, :].rearrange("r p t -> p r t"))
+            if r == 0:
+                nc.sync.dma_start(out=gate_first[:], in_=gate[0, 0:P, :])
+        nc.sync.dma_start(out=gate_rest[:], in_=gate[1:, 0:P, :].rearrange("r p t -> p r t"))
 
         for part, (first, end, on_vector) in zip(x_loaded, X_LOADS):
             rounded = keep.tile([P, end - first, PACK], BF16, name=f"rounded_{first}", align_bytes=64)
@@ -208,35 +214,34 @@ def tile_moe_tk_glu_gelu_kernel(
                 )
 
         def turn(j):
-            h_turned[j] = bank(bank_a(turned_after[j]), [P, 2, 2, C])
-            for member in range(2):
-                words = h[2 * j + member][:].bitcast(F32)
+            first, end = TURNED[j]
+            h_turned[j] = bank(turn_bank[j], [P, end - first, 2, C])
+            for e in range(first, end):
+                words = h[e][:].bitcast(F32)
                 for u in range(2):
-                    nc.tensor.transpose(h_turned[j][:, member, u, :], words[:, u * P : (u + 1) * P], ident[:])
+                    nc.tensor.transpose(h_turned[j][:, e - first, u, :], words[:, u * P : (u + 1) * P], ident[:])
 
-        for group in QUANTISED:
-            tile = keep.tile([P, len(group) * 2 * C * PACK], BF16, name=f"h_packed{group[0]}", align_bytes=64)
-            h_packed[group] = tile
-            for place, j in enumerate(group):
-                h_packed[j] = tile[:, place * 2 * C * PACK : (place + 1) * 2 * C * PACK]
+        for first, end in QUANTISED:
+            h_packed[first] = keep.tile([P, (end - first) * C * PACK], BF16, name=f"h_packed{first}", align_bytes=64)
 
         def pack(j):
+            first, end = TURNED[j]
+            start = max(begin for begin, last in QUANTISED if begin <= first)
+            target = h_packed[start][:, (first - start) * C * PACK : (end - start) * C * PACK]
             (nc.vector.tensor_copy if j in PACKS_ON_VECTOR else nc.scalar.copy)(
-                out=h_packed[j].bitcast(F32).rearrange("p (x s u) -> p x s u", x=2, u=2),
+                out=target.bitcast(F32).rearrange("p (x s u) -> p x s u", s=C, u=2),
                 in_=h_turned[j][:].rearrange("p x u s -> p x s u"),
             )
 
-        def members(group):
-            return [2 * j + member for j in group for member in range(2)]
-
-        def quantise(group):
-            width = len(group) * 2 * C
-            words = keep.tile([P, width], U32, name=f"h_words{group[0]}", align_bytes=64)
-            scales = keep.tile([P, width], U8, name=f"h_scales{group[0]}", align_bytes=64)
-            nc.vector.quantize_mx(out=words[:].bitcast(FP8X4), scales=scales[:], in_=h_packed[group][:])
-            for place, e in enumerate(members(group)):
-                h_words[e] = words[:, columns(place, 0)]
-                h_scales[e] = scales[:, columns(place, 0)]
+        def quantise(first, end):
+            width = (end - first) * C
+            name = f"h_words{first}"
+            words = keep.tile([P, width], U32, name=name, align_bytes=64)
+            scales = keep.tile([P, width], U8, name=f"h_scales{first}", align_bytes=64)
+            nc.vector.quantize_mx(out=words[:].bitcast(FP8X4), scales=scales[:], in_=h_packed[first][:])
+            for e in range(first, end):
+                h_words[e] = words[:, columns(e, first)]
+                h_scales[e] = scales[:, columns(e, first)]
 
         def second_product(e, half, sums):
             nc.tensor.matmul_mx(
@@ -249,30 +254,26 @@ def tile_moe_tk_glu_gelu_kernel(
                 stop=True,
             )
 
-        def second_layer(group):
-            y_run[group] = bank(result_bank[QUANTISED.index(group)], [P, len(group), 2 * C])
-            for place, e in enumerate(members(group)):
-                second_product(e, 0, y_run[group][:, place // 2, columns(place % 2, 0)])
-
-        def results(group, copy):
-            by_pair = y[0][:].rearrange("p (j x) -> p j x", j=PAIRS)
-            copy(out=by_pair[:, group[0] : group[-1] + 1 : max(group[-1] - group[0], 1), :], in_=y_run[group][:])
-
+        turned_at = (5, 7, 10, 12, 12, 12, 13)
+        packed_at = (5, 7, 12, 12, 12, 12, 13)
         for step in range(E + 2):
-            if step in {5: 0, 7: 1}:
-                turn({5: 0, 7: 1}[step])
-                pack({5: 0, 7: 1}[step])
-            for stage, lag in ((multiply, 2), (activate, 1), (first_layer, 0)):
+            for stage, lag in ((multiply, 2), (activate, 1)):
                 if 0 <= step - lag < E:
                     stage(step - lag)
-        for j in (2, 3, 4, 5):
-            turn(j)
-            pack(j)
-        for group in QUANTISED:
-            quantise(group)
-            second_layer(group)
-        for group, copy in zip(QUANTISED, (nc.scalar.copy, nc.scalar.copy, nc.vector.tensor_copy, nc.vector.tensor_copy)):
-            results(group, copy)
+            for stage, steps in ((turn, turned_at), (pack, packed_at)):
+                for j, at in enumerate(steps):
+                    if at == step:
+                        stage(j)
+            if step < E:
+                first_layer(step)
+        for first, end in QUANTISED:
+            quantise(first, end)
+        for number, (first, end) in zip(result_bank, RESULTS):
+            y_run[first] = bank(number, [P, (end - first) * C])
+            for e in range(first, end):
+                second_product(e, 0, y_run[first][:, columns(e, first)])
+        for (first, end), copy in zip(RESULTS, (nc.scalar.copy, nc.scalar.copy, nc.vector.tensor_copy, nc.vector.tensor_copy)):
+            copy(out=y[0][:, first * C : end * C], in_=y_run[first][:])
 
         late_firsts = (E - LATE_RUN, 0, LATE_RUN)
         late_banks = (result_bank[0], result_bank[1], result_bank[3])
@@ -287,19 +288,19 @@ def tile_moe_tk_glu_gelu_kernel(
         turned_sum, three = {}, {}
 
         def fetch(r, half):
-            nc.vector.tensor_tensor(weighted[half][r][:], y[half][:].indirect(pos_t[r][:]), gate_t[:, r, :], MULT)
+            nc.vector.tensor_tensor(weighted[half][r][:], y[half][:].indirect(pos_t[r][:]), gates[r], MULT)
 
         def add_turned(r, half):
             for b in range(BLOCKS):
-                if r == 0:
+                if r == SUMMED[half][0]:
                     turned_sum[half, b] = bank(sum_banks[half][b], [P, P])
                 nc.tensor.matmul(
                     turned_sum[half, b][:],
                     lhsT=weighted[half][r][:, b * P : (b + 1) * P],
                     rhs=ident[:],
                     is_transpose=True,
-                    start=(r == 0),
-                    stop=(r == TOP - 2),
+                    start=(r == SUMMED[half][0]),
+                    stop=(r == SUMMED[half][-1]),
                 )
 
         def turn_back(half):
@@ -310,7 +311,7 @@ def tile_moe_tk_glu_gelu_kernel(
                 nc.tensor.transpose(three[half][:, b * P : (b + 1) * P], staged[:], ident[:])
 
         for half in range(HALVES):
-            for r in range(TOP - 1):
+            for r in SUMMED[half]:
                 fetch(r, half)
                 add_turned(r, half)
             turn_back(half)

@@ -29,12 +29,14 @@ ADD, MULT = mybir.AluOpType.add, mybir.AluOpType.mult
 X_LOADS = [(0, 256, 160), (256, T, 80)]
 
 GATHERS = [(0, 1), (1, 3), (3, 6), (6, 9), (9, E)]
-ON_GPSIMD = 3
+ON_GPSIMD = 2
 TURNED = [(0, 2), (2, 4), (4, 6), (6, 8), (8, 10), (10, 11), (11, 12)]
-QUANTISED = [(0, 4), (4, 8), (8, 10), (10, 12)]
-RESULTS = [(0, 4), (4, 8), (8, 10), (10, 12)]
+QUANTISED = [(0, 4), (4, 8), (8, 10), (10, 11), (11, 12)]
+RESULTS = [(0, 4), (4, 8), (8, 11), (11, 12)]
 PACKS_ON_VECTOR = ()
 SUMMED = ((0, 1, 2), (1, 2, 0))
+BEHIND = {9: 4}
+TAKES = {(1, 0): "weighted01"}
 LATE_RUN = 4
 WORD_LOADS = [(1, 3), (3, 5), (5, 7), (7, 9), (9, E)]
 EARLY_SCALES = 5
@@ -60,7 +62,7 @@ def tile_moe_tk_glu_gelu_kernel(
         def bank_b(e):
             return W3[e % len(W3)]
 
-        turn_bank = (bank_a(3), bank_a(5), bank_a(8), bank_a(9), bank_a(10), bank_a(11), bank_a(8))
+        turn_bank = (bank_a(3), bank_b(3), bank_b(5), bank_a(9), bank_a(10), bank_a(11), bank_a(8))
         result_bank = [bank_b(e) for e in range(E - 4, E)]
 
         offs_t = lists.tile([P, S // PER_COLUMN], U16, name="offs_t")
@@ -73,10 +75,7 @@ def tile_moe_tk_glu_gelu_kernel(
         token_scales = keep.tile([P, WINDOW], U8, name="token_scales", align_bytes=64)
         ident = keep.tile([P, P], F32, name="ident", align_bytes=64)
         y = [keep.tile([P, S], F32, name=f"y{half}", align_bytes=64) for half in range(HALVES)]
-        weighted = [
-            [keep.tile([P, T], F32, name="weighted01" if (half, r) == (1, 0) else f"weighted{half}{r}", align_bytes=64) for r in range(TOP)]
-            for half in range(HALVES)
-        ]
+        weighted = [{}, {}]
 
         nc.vector.memset(token_words[:, T:WINDOW], 0)
         nc.gpsimd.memset(token_scales[:], 0)
@@ -161,16 +160,20 @@ def tile_moe_tk_glu_gelu_kernel(
         def columns(e, first):
             return slice((e - first) * C, (e - first + 1) * C)
 
-        for first, end in GATHERS:
+        def gather(first, end):
             width = (end - first) * C
             entries = offs_t[:, first * C // PER_COLUMN : end * C // PER_COLUMN]
-            scales = keep.tile([P, width], U8, name=f"slot_scales{first}", align_bytes=64)
+            scales = keep.tile([P, width], U8, name=f"gelu_a{BEHIND[first]}" if first in BEHIND else f"slot_scales{first}", align_bytes=64)
             nc.vector.tensor_copy(scales[:], token_scales[:].indirect(entries))
-            words = keep.tile([P, width], U32, name=f"slot_words{first}", align_bytes=64)
+            words = keep.tile([P, width], U32, name=f"gelu_a{BEHIND[first] - 1}" if first in BEHIND else f"slot_words{first}", align_bytes=64)
             nc.vector.tensor_copy(words[:], token_words[:].bitcast(U32).indirect(entries))
             for member in range(first, end):
                 slot_words[member] = words[:, columns(member, first)]
                 slot_scales[member] = scales[:, columns(member, first)]
+
+        for first, end in GATHERS:
+            if first not in BEHIND:
+                gather(first, end)
 
         def first_product(e, sums, words, scales):
             nc.tensor.matmul_mx(
@@ -183,9 +186,14 @@ def tile_moe_tk_glu_gelu_kernel(
                 stop=True,
             )
 
-        def first_layer(e):
+        def w1_product(e):
             sums_a[e] = bank(bank_a(e), [P, H])
             first_product(e, sums_a[e], w1, s1)
+
+        def first_layer(e):
+            for ahead in (e, e + 1):
+                if ahead < E and ahead not in sums_a and (ahead == e or ahead >= 11):
+                    w1_product(ahead)
             sums_b[e] = bank(bank_b(e), [P, H])
             first_product(e, sums_b[e], w3, s3)
 
@@ -235,7 +243,7 @@ def tile_moe_tk_glu_gelu_kernel(
 
         def quantise(first, end):
             width = (end - first) * C
-            name = f"h_words{first}"
+            name = f"gelu_a6" if first == 0 else f"h_words{first}"
             words = keep.tile([P, width], U32, name=name, align_bytes=64)
             scales = keep.tile([P, width], U8, name=f"h_scales{first}", align_bytes=64)
             nc.vector.quantize_mx(out=words[:].bitcast(FP8X4), scales=scales[:], in_=h_packed[first][:])
@@ -254,12 +262,15 @@ def tile_moe_tk_glu_gelu_kernel(
                 stop=True,
             )
 
-        turned_at = (5, 7, 10, 12, 12, 12, 13)
-        packed_at = (5, 7, 12, 12, 12, 12, 13)
+        turned_at = (5, 7, 8, 11, 12, 12, 13)
+        packed_at = (5, 7, 9, 12, 12, 12, 13)
         for step in range(E + 2):
             for stage, lag in ((multiply, 2), (activate, 1)):
                 if 0 <= step - lag < E:
                     stage(step - lag)
+            for first, end in GATHERS:
+                if BEHIND.get(first) == step - 2:
+                    gather(first, end)
             for stage, steps in ((turn, turned_at), (pack, packed_at)):
                 for j, at in enumerate(steps):
                     if at == step:
@@ -272,7 +283,7 @@ def tile_moe_tk_glu_gelu_kernel(
             y_run[first] = bank(number, [P, (end - first) * C])
             for e in range(first, end):
                 second_product(e, 0, y_run[first][:, columns(e, first)])
-        for (first, end), copy in zip(RESULTS, (nc.scalar.copy, nc.scalar.copy, nc.vector.tensor_copy, nc.vector.tensor_copy)):
+        for (first, end), copy in zip(RESULTS, (nc.scalar.copy, nc.vector.tensor_copy, nc.scalar.copy, nc.vector.tensor_copy)):
             copy(out=y[0][:, first * C : end * C], in_=y_run[first][:])
 
         late_firsts = (E - LATE_RUN, 0, LATE_RUN)
@@ -287,8 +298,14 @@ def tile_moe_tk_glu_gelu_kernel(
         back_banks = (bank_a(9), result_bank[2])
         turned_sum, three = {}, {}
 
-        def fetch(r, half):
-            nc.vector.tensor_tensor(weighted[half][r][:], y[half][:].indirect(pos_t[r][:]), gates[r], MULT)
+        def fetch(r, half, first=0, end=T):
+            if first == 0:
+                name = TAKES.get((half, r), f"weighted{half}{r}")
+                weighted[half][r] = keep.tile([P, T], F32, name=name, align_bytes=64)
+            entries = pos_t[r][:, first // PER_COLUMN : end // PER_COLUMN]
+            nc.vector.tensor_tensor(
+                weighted[half][r][:, first:end], y[half][:].indirect(entries), gates[r][:, first:end], MULT
+            )
 
         def add_turned(r, half):
             for b in range(BLOCKS):
@@ -315,14 +332,18 @@ def tile_moe_tk_glu_gelu_kernel(
                 fetch(r, half)
                 add_turned(r, half)
             turn_back(half)
-        for half in range(HALVES):
-            fetch(TOP - 1, half)
-
         pieces = ([(0, T)], [(0, T - P), (T - P, T)])
-        for half in range(HALVES):
-            total = keep.tile([P, T], F32, name=f"total{half}", align_bytes=64)
+        total = [keep.tile([P, T], F32, name=f"total{half}", align_bytes=64) for half in range(HALVES)]
+
+        def finish(half):
             for first, end in pieces[half]:
                 nc.vector.tensor_tensor(
-                    total[:, first:end], three[half][:, first:end], weighted[half][TOP - 1][:, first:end], ADD
+                    total[half][:, first:end], three[half][:, first:end], weighted[half][TOP - 1][:, first:end], ADD
                 )
-                nc.sync.dma_start(out=out[half * P : (half + 1) * P, first:end], in_=total[:, first:end])
+                nc.sync.dma_start(out=out[half * P : (half + 1) * P, first:end], in_=total[half][:, first:end])
+
+        fetch(TOP - 1, 0)
+        fetch(TOP - 1, 1, 0, 256)
+        finish(0)
+        fetch(TOP - 1, 1, 256, T)
+        finish(1)

@@ -108,9 +108,9 @@ def tile_moe_tk_glu_gelu_kernel(
 
         x_rows = xT.rearrange("(p j) t -> p j t", j=PACK)
         x_loaded = []
-        for first, end, on_vector in X_LOADS:
-            part = keep.tile([P, PACK, end - first], F32, name=f"x_{first}", align_bytes=64)
-            nc.sync.dma_start(out=part[:], in_=x_rows[:, :, first:end])
+        for j in (0, 2):
+            part = keep.tile([P, 2, T], F32, name=f"x_{j}", align_bytes=64)
+            nc.sync.dma_start(out=part[:], in_=x_rows[:, j : j + 2, :])
             x_loaded.append(part)
         nc.sync.dma_start(offs_t[:], offs)
         load_words(w1, "w1", w1_words, 0, 1)
@@ -139,16 +139,26 @@ def tile_moe_tk_glu_gelu_kernel(
                 nc.sync.dma_start(out=gate_first[:], in_=gate[0, 0:P, :])
         nc.sync.dma_start(out=gate_rest[:], in_=gate[1:, 0:P, :].rearrange("r p t -> p r t"))
 
-        for part, (first, end, on_vector) in zip(x_loaded, X_LOADS):
-            rounded = keep.tile([P, end - first, PACK], BF16, name=f"rounded_{first}", align_bytes=64)
-            source = part[:].rearrange("p j (c i) -> p c j i", i=4)
-            target = rounded[:].rearrange("p (c i) j -> p c j i", i=4)
-            nc.vector.tensor_copy(out=target[:, : on_vector // 4], in_=source[:, : on_vector // 4])
-            nc.scalar.copy(out=target[:, on_vector // 4 :], in_=source[:, on_vector // 4 :])
+        spans = ((0, 256), (256, T))
+        rounded = [keep.tile([P, end - first, PACK], BF16, name=f"rounded_{first}", align_bytes=64) for first, end in spans]
+        for half, part in enumerate(x_loaded):
+            for span, first, end, copy in (
+                (0, 0, 128, nc.vector.tensor_copy),
+                (0, 128, 256, nc.scalar.copy),
+                (1, 256, T, nc.vector.tensor_copy),
+            ):
+                start = spans[span][0]
+                copy(
+                    out=rounded[span][:, first - start : end - start, 2 * half : 2 * half + 2].rearrange(
+                        "p (c i) j -> p c j i", i=4
+                    ),
+                    in_=part[:, :, first:end].rearrange("p j (c i) -> p c j i", i=4),
+                )
+        for tile, (first, end) in zip(rounded, spans):
             nc.vector.quantize_mx(
                 out=token_words[:, first:end].bitcast(FP8X4),
                 scales=token_scales[:, first:end],
-                in_=rounded[:].rearrange("p t j -> p (t j)"),
+                in_=tile[:].rearrange("p t j -> p (t j)"),
             )
 
         slot_words, slot_scales, h_words, h_scales = {}, {}, {}, {}

@@ -26,20 +26,21 @@ FP4X4 = mybir.dt.float4_e2m1fn_x4
 GELU = mybir.ActivationFunctionType.Gelu_apprx_tanh
 ADD, MULT = mybir.AluOpType.add, mybir.AluOpType.mult
 
-X_LOADS = [(0, 256, 160), (256, T, 80)]
+X_CUT = 2
+ON_SCALAR = P
 
-GATHERS = [(0, 1), (1, 3), (3, 6), (6, 9), (9, E)]
+GATHERS = [(0, 1), (1, 3), (3, 6), (6, 9)]
+LATE_GATHER = (9, E)
 ON_GPSIMD = 2
-TURNED = [(0, 2), (2, 4), (4, 6), (6, 8), (8, 10), (10, 11), (11, 12)]
-QUANTISED = [(0, 4), (4, 8), (8, 10), (10, 11), (11, 12)]
-RESULTS = [(0, 4), (4, 8), (8, 11), (11, 12)]
-PACKS_ON_VECTOR = ()
-SUMMED = ((0, 1, 2), (1, 2, 0))
-BEHIND = {9: 4}
-TAKES = {(1, 0): "weighted01"}
-LATE_RUN = 4
-WORD_LOADS = [(1, 3), (3, 5), (5, 7), (7, 9), (9, E)]
 EARLY_SCALES = 5
+
+TURNED = [(0, 2), (2, 4), (4, 6), (6, 8), (8, 10), (10, 11), (11, E)]
+QUANTISED = [(0, 4), (4, 8), (8, 10), (10, 11), (11, E)]
+RESULTS = [(0, 4), (4, 8), (8, 11), (11, E)]
+EARLY_PACKS = 3
+LATE_RUN = 4
+
+SUMMED = ((0, 1, 2), (1, 2, 0))
 
 
 def tile_moe_tk_glu_gelu_kernel(
@@ -75,7 +76,6 @@ def tile_moe_tk_glu_gelu_kernel(
         token_scales = keep.tile([P, WINDOW], U8, name="token_scales", align_bytes=64)
         ident = keep.tile([P, P], F32, name="ident", align_bytes=64)
         y = [keep.tile([P, S], F32, name=f"y{half}", align_bytes=64) for half in range(HALVES)]
-        weighted = [{}, {}]
 
         nc.vector.memset(token_words[:, T:WINDOW], 0)
         nc.gpsimd.memset(token_scales[:], 0)
@@ -108,53 +108,44 @@ def tile_moe_tk_glu_gelu_kernel(
 
         x_rows = xT.rearrange("(p j) t -> p j t", j=PACK)
         x_loaded = []
-        for j in (0, 2):
-            part = keep.tile([P, 2, T], F32, name=f"x_{j}", align_bytes=64)
-            nc.sync.dma_start(out=part[:], in_=x_rows[:, j : j + 2, :])
+        for j in (0, X_CUT):
+            part = keep.tile([P, X_CUT, T], F32, name=f"x_{j}", align_bytes=64)
+            nc.sync.dma_start(out=part[:], in_=x_rows[:, j : j + X_CUT, :])
             x_loaded.append(part)
         nc.sync.dma_start(offs_t[:], offs)
         load_words(w1, "w1", w1_words, 0, 1)
-        load_scales(s1, "s1", w1_scales, 0, 5)
+        load_scales(s1, "s1", w1_scales, 0, EARLY_SCALES)
         load_words(w3, "w3", w3_words, 0, 1)
-        load_scales(s3, "s3", w3_scales, 0, 5)
-        load_words(w1, "w1", w1_words, 1, 3)
-        load_words(w3, "w3", w3_words, 1, 3)
-        load_scales(s1, "s1", w1_scales, 5, 12)
-        load_words(w1, "w1", w1_words, 3, 5)
-        load_words(w3, "w3", w3_words, 3, 5)
-        load_scales(s3, "s3", w3_scales, 5, 12)
-        load_words(w1, "w1", w1_words, 5, 7)
-        load_words(w3, "w3", w3_words, 5, 7)
-        load_words(w1, "w1", w1_words, 7, 9)
-        load_words(w3, "w3", w3_words, 7, 9)
-        load_words(w1, "w1", w1_words, 9, 12)
-        load_words(w3, "w3", w3_words, 9, 11)
-        load_words(w3, "w3", w3_words, 11, 12)
-        load_scales(s2, "s2", w2_scales, 0, 12)
-        load_words(w2, "w2", w2_words, 0, 8)
-        load_words(w2, "w2", w2_words, 8, 12)
-        for r, pos in enumerate((pos1, pos2, pos3, pos4)):
-            nc.sync.dma_start(pos_t[r][:], pos)
-            if r == 0:
-                nc.sync.dma_start(out=gate_first[:], in_=gate[0, 0:P, :])
+        load_scales(s3, "s3", w3_scales, 0, EARLY_SCALES)
+        load_first_layer_words(1, 3)
+        load_scales(s1, "s1", w1_scales, EARLY_SCALES, E)
+        load_first_layer_words(3, EARLY_SCALES)
+        load_scales(s3, "s3", w3_scales, EARLY_SCALES, E)
+        load_first_layer_words(5, 7)
+        load_first_layer_words(7, 9)
+        load_words(w1, "w1", w1_words, 9, E)
+        load_words(w3, "w3", w3_words, 9, E - 1)
+        load_words(w3, "w3", w3_words, E - 1, E)
+        load_scales(s2, "s2", w2_scales, 0, E)
+        load_words(w2, "w2", w2_words, 0, 2 * LATE_RUN)
+        load_words(w2, "w2", w2_words, 2 * LATE_RUN, E)
+        nc.sync.dma_start(pos_t[0][:], pos1)
+        nc.sync.dma_start(out=gate_first[:], in_=gate[0, 0:P, :])
+        for tile, pos in zip(pos_t[1:], (pos2, pos3, pos4)):
+            nc.sync.dma_start(tile[:], pos)
         nc.sync.dma_start(out=gate_rest[:], in_=gate[1:, 0:P, :].rearrange("r p t -> p r t"))
 
-        spans = ((0, 256), (256, T))
-        rounded = [keep.tile([P, end - first, PACK], BF16, name=f"rounded_{first}", align_bytes=64) for first, end in spans]
-        for half, part in enumerate(x_loaded):
-            for span, first, end, copy in (
-                (0, 0, 128, nc.vector.tensor_copy),
-                (0, 128, 256, nc.scalar.copy),
-                (1, 256, T, nc.vector.tensor_copy),
-            ):
-                start = spans[span][0]
+        shares = ((0, ON_SCALAR, nc.scalar.copy), (ON_SCALAR, T, nc.vector.tensor_copy))
+        rounded = [
+            keep.tile([P, end - first, PACK], BF16, name=f"rounded_{first}", align_bytes=64) for first, end, _ in shares
+        ]
+        for j, part in zip((0, X_CUT), x_loaded):
+            for tile, (first, end, copy) in zip(rounded, shares):
                 copy(
-                    out=rounded[span][:, first - start : end - start, 2 * half : 2 * half + 2].rearrange(
-                        "p (c i) j -> p c j i", i=4
-                    ),
+                    out=tile[:, :, j : j + X_CUT].rearrange("p (c i) j -> p c j i", i=4),
                     in_=part[:, :, first:end].rearrange("p j (c i) -> p c j i", i=4),
                 )
-        for tile, (first, end) in zip(rounded, spans):
+        for tile, (first, end, _) in zip(rounded, shares):
             nc.vector.quantize_mx(
                 out=token_words[:, first:end].bitcast(FP8X4),
                 scales=token_scales[:, first:end],
@@ -164,26 +155,22 @@ def tile_moe_tk_glu_gelu_kernel(
         slot_words, slot_scales, h_words, h_scales = {}, {}, {}, {}
         sums_a, sums_b, gelu_a, staged_b, h, h_turned, h_packed, y_run = {}, {}, {}, {}, {}, {}, {}, {}
 
-        def ending_at(spans, e):
-            return [(first, end) for first, end in spans if end - 1 == e]
-
         def columns(e, first):
             return slice((e - first) * C, (e - first + 1) * C)
 
-        def gather(first, end):
+        def gather(first, end, scales_in, words_in):
             width = (end - first) * C
             entries = offs_t[:, first * C // PER_COLUMN : end * C // PER_COLUMN]
-            scales = keep.tile([P, width], U8, name=f"gelu_a{BEHIND[first]}" if first in BEHIND else f"slot_scales{first}", align_bytes=64)
+            scales = keep.tile([P, width], U8, name=scales_in, align_bytes=64)
             nc.vector.tensor_copy(scales[:], token_scales[:].indirect(entries))
-            words = keep.tile([P, width], U32, name=f"gelu_a{BEHIND[first] - 1}" if first in BEHIND else f"slot_words{first}", align_bytes=64)
+            words = keep.tile([P, width], U32, name=words_in, align_bytes=64)
             nc.vector.tensor_copy(words[:], token_words[:].bitcast(U32).indirect(entries))
             for member in range(first, end):
                 slot_words[member] = words[:, columns(member, first)]
                 slot_scales[member] = scales[:, columns(member, first)]
 
         for first, end in GATHERS:
-            if first not in BEHIND:
-                gather(first, end)
+            gather(first, end, f"slot_scales{first}", f"slot_words{first}")
 
         def first_product(e, sums, words, scales):
             nc.tensor.matmul_mx(
@@ -200,10 +187,7 @@ def tile_moe_tk_glu_gelu_kernel(
             sums_a[e] = bank(bank_a(e), [P, H])
             first_product(e, sums_a[e], w1, s1)
 
-        def first_layer(e):
-            for ahead in (e, e + 1):
-                if ahead < E and ahead not in sums_a and (ahead == e or ahead >= 11):
-                    w1_product(ahead)
+        def w3_product(e):
             sums_b[e] = bank(bank_b(e), [P, H])
             first_product(e, sums_b[e], w3, s3)
 
@@ -216,14 +200,12 @@ def tile_moe_tk_glu_gelu_kernel(
         def activate(e):
             gelu_a[e] = keep.tile([P, H], F32, name=f"gelu_a{e}", align_bytes=64)
             nc.scalar.activation(out=by_pairs(gelu_a[e]), in_=from_sums(sums_a[e]), func=GELU)
-
             if e < ON_GPSIMD:
                 staged_b[e] = keep.tile([P, H], F32, name=f"staged_b{e}", align_bytes=64)
                 nc.scalar.copy(out=by_pairs(staged_b[e]), in_=from_sums(sums_b[e]))
 
         def multiply(e):
-            name = "h0" if e == 0 else f"h{e}"
-            h[e] = keep.tile([P, H], BF16, name=name, align_bytes=64)
+            h[e] = keep.tile([P, H], BF16, name=f"h{e}", align_bytes=64)
             if e < ON_GPSIMD:
                 nc.gpsimd.tensor_tensor(out=h[e][:], in0=staged_b[e][:], in1=gelu_a[e][:], op=MULT)
             else:
@@ -246,14 +228,14 @@ def tile_moe_tk_glu_gelu_kernel(
             first, end = TURNED[j]
             start = max(begin for begin, last in QUANTISED if begin <= first)
             target = h_packed[start][:, (first - start) * C * PACK : (end - start) * C * PACK]
-            (nc.vector.tensor_copy if j in PACKS_ON_VECTOR else nc.scalar.copy)(
+            nc.scalar.copy(
                 out=target.bitcast(F32).rearrange("p (x s u) -> p x s u", s=C, u=2),
                 in_=h_turned[j][:].rearrange("p x u s -> p x s u"),
             )
 
         def quantise(first, end):
             width = (end - first) * C
-            name = f"gelu_a6" if first == 0 else f"h_words{first}"
+            name = "gelu_a6" if first == 0 else f"h_words{first}"
             words = keep.tile([P, width], U32, name=name, align_bytes=64)
             scales = keep.tile([P, width], U8, name=f"h_scales{first}", align_bytes=64)
             nc.vector.quantize_mx(out=words[:].bitcast(FP8X4), scales=scales[:], in_=h_packed[first][:])
@@ -272,28 +254,36 @@ def tile_moe_tk_glu_gelu_kernel(
                 stop=True,
             )
 
-        turned_at = (5, 7, 8, 11, 12, 12, 13)
-        packed_at = (5, 7, 9, 12, 12, 12, 13)
+        turned_in = {end + 2: j for j, (first, end) in enumerate(TURNED[: EARLY_PACKS + 1])}
+        packed_in = {end + 3: j for j, (first, end) in enumerate(TURNED[:EARLY_PACKS])}
         for step in range(E + 2):
             for stage, lag in ((multiply, 2), (activate, 1)):
                 if 0 <= step - lag < E:
                     stage(step - lag)
-            for first, end in GATHERS:
-                if BEHIND.get(first) == step - 2:
-                    gather(first, end)
-            for stage, steps in ((turn, turned_at), (pack, packed_at)):
-                for j, at in enumerate(steps):
-                    if at == step:
-                        stage(j)
+            if step - 2 == 4:
+                gather(*LATE_GATHER, "gelu_a4", "gelu_a3")
+            if step in turned_in:
+                turn(turned_in[step])
+            if step in packed_in:
+                pack(packed_in[step])
+            if step < E - 1:
+                w1_product(step)
+            if step == E - 2:
+                w1_product(E - 1)
             if step < E:
-                first_layer(step)
+                w3_product(step)
+        pack(EARLY_PACKS)
+        for j in range(EARLY_PACKS + 1, len(TURNED)):
+            turn(j)
+            pack(j)
         for first, end in QUANTISED:
             quantise(first, end)
         for number, (first, end) in zip(result_bank, RESULTS):
             y_run[first] = bank(number, [P, (end - first) * C])
             for e in range(first, end):
                 second_product(e, 0, y_run[first][:, columns(e, first)])
-        for (first, end), copy in zip(RESULTS, (nc.scalar.copy, nc.vector.tensor_copy, nc.scalar.copy, nc.vector.tensor_copy)):
+        for run, (first, end) in enumerate(RESULTS):
+            copy = nc.vector.tensor_copy if run % 2 else nc.scalar.copy
             copy(out=y[0][:, first * C : end * C], in_=y_run[first][:])
 
         late_firsts = (E - LATE_RUN, 0, LATE_RUN)
@@ -306,15 +296,15 @@ def tile_moe_tk_glu_gelu_kernel(
 
         sum_banks = ([bank_a(8), bank_a(10), bank_a(11)], late_banks)
         back_banks = (bank_a(9), result_bank[2])
-        turned_sum, three = {}, {}
+        weighted, turned_sum, three = {}, {}, {}
 
         def fetch(r, half, first=0, end=T):
             if first == 0:
-                name = TAKES.get((half, r), f"weighted{half}{r}")
-                weighted[half][r] = keep.tile([P, T], F32, name=name, align_bytes=64)
+                name = "weighted01" if (half, r) == (1, 0) else f"weighted{half}{r}"
+                weighted[half, r] = keep.tile([P, T], F32, name=name, align_bytes=64)
             entries = pos_t[r][:, first // PER_COLUMN : end // PER_COLUMN]
             nc.vector.tensor_tensor(
-                weighted[half][r][:, first:end], y[half][:].indirect(entries), gates[r][:, first:end], MULT
+                weighted[half, r][:, first:end], y[half][:].indirect(entries), gates[r][:, first:end], MULT
             )
 
         def add_turned(r, half):
@@ -323,7 +313,7 @@ def tile_moe_tk_glu_gelu_kernel(
                     turned_sum[half, b] = bank(sum_banks[half][b], [P, P])
                 nc.tensor.matmul(
                     turned_sum[half, b][:],
-                    lhsT=weighted[half][r][:, b * P : (b + 1) * P],
+                    lhsT=weighted[half, r][:, b * P : (b + 1) * P],
                     rhs=ident[:],
                     is_transpose=True,
                     start=(r == SUMMED[half][0]),
@@ -348,12 +338,12 @@ def tile_moe_tk_glu_gelu_kernel(
         def finish(half):
             for first, end in pieces[half]:
                 nc.vector.tensor_tensor(
-                    total[half][:, first:end], three[half][:, first:end], weighted[half][TOP - 1][:, first:end], ADD
+                    total[half][:, first:end], three[half][:, first:end], weighted[half, TOP - 1][:, first:end], ADD
                 )
                 nc.sync.dma_start(out=out[half * P : (half + 1) * P, first:end], in_=total[half][:, first:end])
 
         fetch(TOP - 1, 0)
-        fetch(TOP - 1, 1, 0, 256)
+        fetch(TOP - 1, 1, 0, T - P)
         finish(0)
-        fetch(TOP - 1, 1, 256, T)
+        fetch(TOP - 1, 1, T - P, T)
         finish(1)

@@ -24,6 +24,7 @@ U8 = mybir.dt.uint8
 FP8X4 = mybir.dt.float8_e4m3fn_x4
 FP4X4 = mybir.dt.float4_e2m1fn_x4
 GELU = mybir.ActivationFunctionType.Gelu_apprx_tanh
+COPY = mybir.ActivationFunctionType.Copy
 ADD, MULT = mybir.AluOpType.add, mybir.AluOpType.mult
 
 X_CUT = 2
@@ -40,7 +41,7 @@ RESULTS = [(0, 4), (4, 8), (8, 11), (11, E)]
 EARLY_PACKS = 3
 LATE_RUN = 4
 
-SUMMED = ((0, 1, 2), (1, 2, 0))
+SUMMED = ((0, 1, 2), (0, 1, 2))
 
 
 def tile_moe_tk_glu_gelu_kernel(
@@ -69,9 +70,8 @@ def tile_moe_tk_glu_gelu_kernel(
         offs_t = lists.tile([P, S // PER_COLUMN], U16, name="offs_t")
         pos_t = [lists.tile([P, T // PER_COLUMN], U16, name=f"pos_t{r}") for r in range(TOP)]
 
-        gate_first = keep.tile([P, T], F32, name="gate_first", align_bytes=64)
-        gate_rest = keep.tile([P, TOP - 1, T], F32, name="gate_rest", align_bytes=64)
-        gates = [gate_first[:]] + [gate_rest[:, r, :] for r in range(TOP - 1)]
+        gate_t = keep.tile([P, TOP, T], F32, name="gate_t", align_bytes=64)
+        gates = [gate_t[:, r, :] for r in range(TOP)]
         token_words = keep.tile([P, WINDOW], I32, name="token_words", align_bytes=64)
         token_scales = keep.tile([P, WINDOW], U8, name="token_scales", align_bytes=64)
         ident = keep.tile([P, P], F32, name="ident", align_bytes=64)
@@ -129,11 +129,9 @@ def tile_moe_tk_glu_gelu_kernel(
         load_scales(s2, "s2", w2_scales, 0, E)
         load_words(w2, "w2", w2_words, 0, 2 * LATE_RUN)
         load_words(w2, "w2", w2_words, 2 * LATE_RUN, E)
-        nc.sync.dma_start(pos_t[0][:], pos1)
-        nc.sync.dma_start(out=gate_first[:], in_=gate[0, 0:P, :])
-        for tile, pos in zip(pos_t[1:], (pos2, pos3, pos4)):
+        for tile, pos in zip(pos_t, (pos1, pos2, pos3, pos4)):
             nc.sync.dma_start(tile[:], pos)
-        nc.sync.dma_start(out=gate_rest[:], in_=gate[1:, 0:P, :].rearrange("r p t -> p r t"))
+        nc.sync.dma_start(out=gate_t[:], in_=gate[:, 0:P, :].rearrange("r p t -> p r t"))
 
         shares = ((0, ON_SCALAR, nc.scalar.copy), (ON_SCALAR, T, nc.vector.tensor_copy))
         rounded = [
@@ -286,26 +284,35 @@ def tile_moe_tk_glu_gelu_kernel(
             copy = nc.vector.tensor_copy if run % 2 else nc.scalar.copy
             copy(out=y[0][:, first * C : end * C], in_=y_run[first][:])
 
-        late_firsts = (E - LATE_RUN, 0, LATE_RUN)
-        late_banks = (result_bank[0], result_bank[1], result_bank[3])
+        late_firsts = (0, LATE_RUN, E - LATE_RUN)
+        late_banks = (bank_a(9), bank_a(10), bank_a(11))
         for first, number in zip(late_firsts, late_banks):
             late = bank(number, [P, LATE_RUN * C])
             for member in range(first, first + LATE_RUN):
                 second_product(member, 1, late[:, columns(member, first)])
             nc.scalar.copy(out=y[1][:, first * C : (first + LATE_RUN) * C], in_=late[:])
 
-        sum_banks = ([bank_a(8), bank_a(10), bank_a(11)], late_banks)
-        back_banks = (bank_a(9), result_bank[2])
-        weighted, turned_sum, three = {}, {}, {}
+        sum_banks = (result_bank[:BLOCKS], late_banks)
+        back_banks = (result_bank[BLOCKS], bank_a(8))
+        weighted, turned_sum, three, plain = {}, {}, {}, {}
 
         def fetch(r, half, first=0, end=T):
             if first == 0:
-                name = "weighted01" if (half, r) == (1, 0) else f"weighted{half}{r}"
+                name = f"weighted{half}{r}"
                 weighted[half, r] = keep.tile([P, T], F32, name=name, align_bytes=64)
             entries = pos_t[r][:, first // PER_COLUMN : end // PER_COLUMN]
             nc.vector.tensor_tensor(
                 weighted[half, r][:, first:end], y[half][:].indirect(entries), gates[r][:, first:end], MULT
             )
+
+        def fetch_plain(r, half):
+            name = f"plain{half}{1 + (r - 1) % 2}"
+            plain[half, r] = keep.tile([P, T], F32, name=name, align_bytes=64)
+            nc.scalar.activation(plain[half, r][:], y[half][:].indirect(pos_t[r][:]), COPY)
+
+        def weigh(r, half):
+            weighted[half, r] = keep.tile([P, T], F32, name=f"weighted{half}{r}", align_bytes=64)
+            nc.vector.tensor_tensor(weighted[half, r][:], plain[half, r][:], gates[r], MULT)
 
         def add_turned(r, half):
             for b in range(BLOCKS):
@@ -320,18 +327,33 @@ def tile_moe_tk_glu_gelu_kernel(
                     stop=(r == SUMMED[half][-1]),
                 )
 
+        staged = {}
+
+        def stage(half):
+            for b in range(BLOCKS):
+                staged[half, b] = keep.tile([P, P], F32, name=f"staged{half}{b}", align_bytes=64)
+                nc.scalar.copy(out=staged[half, b][:], in_=turned_sum[half, b][:])
+
         def turn_back(half):
             three[half] = bank(back_banks[half], [P, T])
             for b in range(BLOCKS):
-                staged = keep.tile([P, P], F32, name=f"staged{half}{b}", align_bytes=64)
-                nc.scalar.copy(out=staged[:], in_=turned_sum[half, b][:])
-                nc.tensor.transpose(three[half][:, b * P : (b + 1) * P], staged[:], ident[:])
+                nc.tensor.transpose(three[half][:, b * P : (b + 1) * P], staged[half, b][:], ident[:])
 
+        for r in range(1, TOP - 1):
+            fetch_plain(r, 1)
         for half in range(HALVES):
             for r in SUMMED[half]:
-                fetch(r, half)
+                if (half, r) in plain:
+                    weigh(r, half)
+                else:
+                    fetch(r, half)
                 add_turned(r, half)
-            turn_back(half)
+            if half == 0:
+                stage(0)
+        fetch_plain(TOP - 1, 1)
+        turn_back(0)
+        stage(1)
+        turn_back(1)
         pieces = ([(0, T)], [(0, T - P), (T - P, T)])
         total = [keep.tile([P, T], F32, name=f"total{half}", align_bytes=64) for half in range(HALVES)]
 
@@ -343,7 +365,6 @@ def tile_moe_tk_glu_gelu_kernel(
                 nc.sync.dma_start(out=out[half * P : (half + 1) * P, first:end], in_=total[half][:, first:end])
 
         fetch(TOP - 1, 0)
-        fetch(TOP - 1, 1, 0, T - P)
+        weigh(TOP - 1, 1)
         finish(0)
-        fetch(TOP - 1, 1, T - P, T)
         finish(1)

@@ -115,9 +115,9 @@ def tile_moe_tk_glu_gelu_kernel(
         nc.sync.dma_start(offs_t[:], offs)
         load_words(w1, "w1", w1_words, 0, 1)
         load_scales(s1, "s1", w1_scales, 0, EARLY_SCALES)
-        load_words(w3, "w3", w3_words, 0, 1)
+        load_words(w3, "w3", w3_words, 0, 3)
         load_scales(s3, "s3", w3_scales, 0, EARLY_SCALES)
-        load_first_layer_words(1, 3)
+        load_words(w1, "w1", w1_words, 1, 3)
         load_scales(s1, "s1", w1_scales, EARLY_SCALES, E)
         load_first_layer_words(3, EARLY_SCALES)
         load_scales(s3, "s3", w3_scales, EARLY_SCALES, E)

@@ -133,7 +133,11 @@ def tile_moe_tk_glu_gelu_kernel(
             nc.sync.dma_start(tile[:], pos)
         nc.sync.dma_start(out=gate_t[:], in_=gate[:, 0:P, :].rearrange("r p t -> p r t"))
 
-        shares = ((0, ON_SCALAR, nc.scalar.copy), (ON_SCALAR, T, nc.vector.tensor_copy))
+        shares = (
+            (P, 2 * P, nc.vector.tensor_copy),
+            (0, ON_SCALAR, nc.scalar.copy),
+            (2 * P, T, nc.vector.tensor_copy),
+        )
         rounded = [
             keep.tile([P, end - first, PACK], BF16, name=f"rounded_{first}", align_bytes=64) for first, end, _ in shares
         ]

@@ -41,7 +41,8 @@ RESULTS = [(0, 4), (4, 8), (8, 11), (11, E)]
 EARLY_PACKS = 3
 LATE_RUN = 4
 
-SUMMED = ((0, 1, 2), (0, 1, 2))
+SUMMED = ((0, 1, 2), (1, 2, 3))
+ADDED = (3, 0)
 
 
 def tile_moe_tk_glu_gelu_kernel(
@@ -70,8 +71,9 @@ def tile_moe_tk_glu_gelu_kernel(
         offs_t = lists.tile([P, S // PER_COLUMN], U16, name="offs_t")
         pos_t = [lists.tile([P, T // PER_COLUMN], U16, name=f"pos_t{r}") for r in range(TOP)]
 
-        gate_t = keep.tile([P, TOP, T], F32, name="gate_t", align_bytes=64)
-        gates = [gate_t[:, r, :] for r in range(TOP)]
+        gate_first = keep.tile([P, T], F32, name="gate_first", align_bytes=64)
+        gate_rest = keep.tile([P, TOP - 1, T], F32, name="gate_rest", align_bytes=64)
+        gates = [gate_first[:]] + [gate_rest[:, r, :] for r in range(TOP - 1)]
         token_words = keep.tile([P, WINDOW], I32, name="token_words", align_bytes=64)
         token_scales = keep.tile([P, WINDOW], U8, name="token_scales", align_bytes=64)
         ident = keep.tile([P, P], F32, name="ident", align_bytes=64)
@@ -131,7 +133,8 @@ def tile_moe_tk_glu_gelu_kernel(
         load_words(w2, "w2", w2_words, 2 * LATE_RUN, E)
         for tile, pos in zip(pos_t, (pos1, pos2, pos3, pos4)):
             nc.sync.dma_start(tile[:], pos)
-        nc.sync.dma_start(out=gate_t[:], in_=gate[:, 0:P, :].rearrange("r p t -> p r t"))
+        nc.sync.dma_start(out=gate_first[:], in_=gate[0, 0:P, :])
+        nc.sync.dma_start(out=gate_rest[:], in_=gate[1:, 0:P, :].rearrange("r p t -> p r t"))
 
         shares = (
             (P, 2 * P, nc.vector.tensor_copy),
@@ -310,7 +313,7 @@ def tile_moe_tk_glu_gelu_kernel(
             )
 
         def fetch_plain(r, half):
-            name = f"plain{half}{1 + (r - 1) % 2}"
+            name = f"plain{half}{r % 2}"
             plain[half, r] = keep.tile([P, T], F32, name=name, align_bytes=64)
             nc.scalar.activation(plain[half, r][:], y[half][:].indirect(pos_t[r][:]), COPY)
 
@@ -343,7 +346,7 @@ def tile_moe_tk_glu_gelu_kernel(
             for b in range(BLOCKS):
                 nc.tensor.transpose(three[half][:, b * P : (b + 1) * P], staged[half, b][:], ident[:])
 
-        for r in range(1, TOP - 1):
+        for r in SUMMED[1][1:]:
             fetch_plain(r, 1)
         for half in range(HALVES):
             for r in SUMMED[half]:
@@ -354,7 +357,7 @@ def tile_moe_tk_glu_gelu_kernel(
                 add_turned(r, half)
             if half == 0:
                 stage(0)
-        fetch_plain(TOP - 1, 1)
+        fetch_plain(ADDED[1], 1)
         turn_back(0)
         stage(1)
         turn_back(1)
@@ -364,11 +367,11 @@ def tile_moe_tk_glu_gelu_kernel(
         def finish(half):
             for first, end in pieces[half]:
                 nc.vector.tensor_tensor(
-                    total[half][:, first:end], three[half][:, first:end], weighted[half, TOP - 1][:, first:end], ADD
+                    total[half][:, first:end], three[half][:, first:end], weighted[half, ADDED[half]][:, first:end], ADD
                 )
                 nc.sync.dma_start(out=out[half * P : (half + 1) * P, first:end], in_=total[half][:, first:end])
 
-        fetch(TOP - 1, 0)
-        weigh(TOP - 1, 1)
+        fetch(ADDED[0], 0)
+        weigh(ADDED[1], 1)
         finish(0)
         finish(1)

from contextlib import ExitStack

import concourse.mybir as mybir
from concourse.masks import make_identity

K, T, E, C, H, N = 512, 384, 12, 128, 512, 256
TOP = 4
S = E * C
P = 128
HALVES = N // P
BLOCKS = T // P
PACK = 4
PER_COLUMN = 16
WINDOW = 512

FLOPS = 2 * S * (2 * K * H + H * N)

F32 = mybir.dt.float32
BF16 = mybir.dt.bfloat16
I32 = mybir.dt.int32
U32 = mybir.dt.uint32
U16 = mybir.dt.uint16
U8 = mybir.dt.uint8
FP8X4 = mybir.dt.float8_e4m3fn_x4
FP4X4 = mybir.dt.float4_e2m1fn_x4
GELU = mybir.ActivationFunctionType.Gelu_apprx_tanh
COPY = mybir.ActivationFunctionType.Copy
ADD, MULT = mybir.AluOpType.add, mybir.AluOpType.mult

X_CUT = 2
ON_SCALAR = P

GATHERS = [(0, 1), (1, 3), (3, 6), (6, 9)]
LATE_GATHER = (9, E)
ON_GPSIMD = 2
EARLY_SCALES = 5

TURNED = [(0, 2), (2, 4), (4, 6), (6, 8), (8, 10), (10, 11), (11, E)]
QUANTISED = [(0, 4), (4, 8), (8, 10), (10, 11), (11, E)]
RESULTS = [(0, 4), (4, 8), (8, 11), (11, E)]
EARLY_PACKS = 3
LATE_RUN = 4

SUMMED = ((0, 1, 2), (1, 2, 3))
ADDED = (3, 0)


def tile_moe_tk_glu_gelu_kernel(
    tc, xT, w1_words, w1_scales, w3_words, w3_scales, w2_words, w2_scales, gate, offs, pos1, pos2, pos3, pos4, out
):
    nc = tc.nc
    with ExitStack() as ctx:
        lists = ctx.enter_context(tc.tile_pool(name="lists", bufs=1))
        keep = ctx.enter_context(tc.tile_pool(name="keep", bufs=1))
        psum = ctx.enter_context(tc.psum_pool(name="psum", bufs=1))

        W1, W3 = (0, 1, 5, 7), (2, 3, 4, 6)

        def bank(number, shape):
            return psum.tile(shape, F32, name=f"bank{number}")

        def bank_a(e):
            return W1[e % len(W1)]

        def bank_b(e):
            return W3[e % len(W3)]

        turn_bank = (bank_a(3), bank_b(3), bank_b(5), bank_a(9), bank_a(10), bank_a(11), bank_a(8))
        result_bank = [bank_b(e) for e in range(E - 4, E)]

        offs_t = lists.tile([P, S // PER_COLUMN], U16, name="offs_t")
        pos_t = [lists.tile([P, T // PER_COLUMN], U16, name=f"pos_t{r}") for r in range(TOP)]

        gate_first = keep.tile([P, T], F32, name="gate_first", align_bytes=64)
        gate_rest = keep.tile([P, TOP - 1, T], F32, name="gate_rest", align_bytes=64)
        gates = [gate_first[:]] + [gate_rest[:, r, :] for r in range(TOP - 1)]
        token_words = keep.tile([P, WINDOW], I32, name="token_words", align_bytes=64)
        token_scales = keep.tile([P, WINDOW], U8, name="token_scales", align_bytes=64)
        ident = keep.tile([P, P], F32, name="ident", align_bytes=64)
        y = [keep.tile([P, S], F32, name=f"y{half}", align_bytes=64) for half in range(HALVES)]

        nc.vector.memset(token_words[:, T:WINDOW], 0)
        nc.gpsimd.memset(token_scales[:], 0)
        make_identity(nc, ident[:])

        w1, w3, w2, s1, s3, s2 = {}, {}, {}, {}, {}, {}

        def load_words(held, tag, words, first, end):
            tile = keep.tile([P, end - first, words.shape[3]], U8, name=f"{tag}_{first}", align_bytes=64)
            nc.sync.dma_start(
                out=tile[:].bitcast(I32),
                in_=words[first:end, 0, :, :].rearrange("e p n -> p e n").bitcast(I32),
            )
            for e in range(first, end):
                held[e] = tile[:, e - first, :]

        def load_scales(held, tag, scales, first, end):
            tile = keep.tile([P, end - first, scales.shape[3]], U8, name=f"{tag}_{first}", align_bytes=64)
            for r in range(4):
                nc.sync.dma_start(
                    out=tile[r:P:32, :, :].bitcast(I32),
                    in_=scales[first:end, 0, r:16:4, :].rearrange("e q n -> q e n").bitcast(I32),
                )
            for e in range(first, end):
                held[e] = tile[:, e - first, :]

        def load_first_layer_words(first, end):
            load_words(w1, "w1", w1_words, first, end)
            load_words(w3, "w3", w3_words, first, end)

        x_rows = xT.rearrange("(p j) t -> p j t", j=PACK)
        x_loaded = []
        for j in (0, X_CUT):
            part = keep.tile([P, X_CUT, T], F32, name=f"x_{j}", align_bytes=64)
            nc.sync.dma_start(out=part[:], in_=x_rows[:, j : j + X_CUT, :])
            x_loaded.append(part)
        nc.sync.dma_start(offs_t[:], offs)
        load_words(w1, "w1", w1_words, 0, 1)
        load_scales(s1, "s1", w1_scales, 0, EARLY_SCALES)
        load_words(w3, "w3", w3_words, 0, 3)
        load_scales(s3, "s3", w3_scales, 0, EARLY_SCALES)
        load_words(w1, "w1", w1_words, 1, 3)
        load_scales(s1, "s1", w1_scales, EARLY_SCALES, E)
        load_first_layer_words(3, EARLY_SCALES)
        load_scales(s3, "s3", w3_scales, EARLY_SCALES, E)
        load_first_layer_words(5, 7)
        load_first_layer_words(7, 9)
        load_words(w1, "w1", w1_words, 9, E)
        load_words(w3, "w3", w3_words, 9, E - 1)
        load_words(w3, "w3", w3_words, E - 1, E)
        load_scales(s2, "s2", w2_scales, 0, E)
        load_words(w2, "w2", w2_words, 0, 2 * LATE_RUN)
        load_words(w2, "w2", w2_words, 2 * LATE_RUN, E)
        for tile, pos in zip(pos_t, (pos1, pos2, pos3, pos4)):
            nc.sync.dma_start(tile[:], pos)
        nc.sync.dma_start(out=gate_first[:], in_=gate[0, 0:P, :])
        nc.sync.dma_start(out=gate_rest[:], in_=gate[1:, 0:P, :].rearrange("r p t -> p r t"))

        shares = (
            (P, 2 * P, nc.vector.tensor_copy),
            (0, ON_SCALAR, nc.scalar.copy),
            (2 * P, T, nc.vector.tensor_copy),
        )
        rounded = [
            keep.tile([P, end - first, PACK], BF16, name=f"rounded_{first}", align_bytes=64) for first, end, _ in shares
        ]
        for j, part in zip((0, X_CUT), x_loaded):
            for tile, (first, end, copy) in zip(rounded, shares):
                copy(
                    out=tile[:, :, j : j + X_CUT].rearrange("p (c i) j -> p c j i", i=4),
                    in_=part[:, :, first:end].rearrange("p j (c i) -> p c j i", i=4),
                )
        for tile, (first, end, _) in zip(rounded, shares):
            nc.vector.quantize_mx(
                out=token_words[:, first:end].bitcast(FP8X4),
                scales=token_scales[:, first:end],
                in_=tile[:].rearrange("p t j -> p (t j)"),
            )

        slot_words, slot_scales, h_words, h_scales = {}, {}, {}, {}
        sums_a, sums_b, gelu_a, staged_b, h, h_turned, h_packed, y_run = {}, {}, {}, {}, {}, {}, {}, {}

        def columns(e, first):
            return slice((e - first) * C, (e - first + 1) * C)

        def gather(first, end, scales_in, words_in):
            width = (end - first) * C
            entries = offs_t[:, first * C // PER_COLUMN : end * C // PER_COLUMN]
            scales = keep.tile([P, width], U8, name=scales_in, align_bytes=64)
            nc.vector.tensor_copy(scales[:], token_scales[:].indirect(entries))
            words = keep.tile([P, width], U32, name=words_in, align_bytes=64)
            nc.vector.tensor_copy(words[:], token_words[:].bitcast(U32).indirect(entries))
            for member in range(first, end):
                slot_words[member] = words[:, columns(member, first)]
                slot_scales[member] = scales[:, columns(member, first)]

        for first, end in GATHERS:
            gather(first, end, f"slot_scales{first}", f"slot_words{first}")

        def first_product(e, sums, words, scales):
            nc.tensor.matmul_mx(
                out=sums[:],
                lhsT=slot_words[e].bitcast(FP8X4),
                lhsT_scale=slot_scales[e],
                rhs=words[e].bitcast(FP4X4),
                rhs_scale=scales[e],
                start=True,
                stop=True,
            )

        def w1_product(e):
            sums_a[e] = bank(bank_a(e), [P, H])
            first_product(e, sums_a[e], w1, s1)

        def w3_product(e):
            sums_b[e] = bank(bank_b(e), [P, H])
            first_product(e, sums_b[e], w3, s3)

        def from_sums(sums):
            return sums[:].rearrange("p (m u v) -> p u m v", u=2, v=2)

        def by_pairs(tile):
            return tile[:].rearrange("p (u m v) -> p u m v", u=2, v=2)

        def activate(e):
            gelu_a[e] = keep.tile([P, H], F32, name=f"gelu_a{e}", align_bytes=64)
            nc.scalar.activation(out=by_pairs(gelu_a[e]), in_=from_sums(sums_a[e]), func=GELU)
            if e < ON_GPSIMD:
                staged_b[e] = keep.tile([P, H], F32, name=f"staged_b{e}", align_bytes=64)
                nc.scalar.copy(out=by_pairs(staged_b[e]), in_=from_sums(sums_b[e]))

        def multiply(e):
            h[e] = keep.tile([P, H], BF16, name=f"h{e}", align_bytes=64)
            if e < ON_GPSIMD:
                nc.gpsimd.tensor_tensor(out=h[e][:], in0=staged_b[e][:], in1=gelu_a[e][:], op=MULT)
            else:
                nc.vector.tensor_tensor(
                    out=by_pairs(h[e]), in0=from_sums(sums_b[e]), in1=by_pairs(gelu_a[e]), op=MULT
                )

        def turn(j):
            first, end = TURNED[j]
            h_turned[j] = bank(turn_bank[j], [P, end - first, 2, C])
            for e in range(first, end):
                words = h[e][:].bitcast(F32)
                for u in range(2):
                    nc.tensor.transpose(h_turned[j][:, e - first, u, :], words[:, u * P : (u + 1) * P], ident[:])

        for first, end in QUANTISED:
            h_packed[first] = keep.tile([P, (end - first) * C * PACK], BF16, name=f"h_packed{first}", align_bytes=64)

        def pack(j):
            first, end = TURNED[j]
            start = max(begin for begin, last in QUANTISED if begin <= first)
            target = h_packed[start][:, (first - start) * C * PACK : (end - start) * C * PACK]
            nc.scalar.copy(
                out=target.bitcast(F32).rearrange("p (x s u) -> p x s u", s=C, u=2),
                in_=h_turned[j][:].rearrange("p x u s -> p x s u"),
            )

        def quantise(first, end):
            width = (end - first) * C
            name = "gelu_a6" if first == 0 else f"h_words{first}"
            words = keep.tile([P, width], U32, name=name, align_bytes=64)
            scales = keep.tile([P, width], U8, name=f"h_scales{first}", align_bytes=64)
            nc.vector.quantize_mx(out=words[:].bitcast(FP8X4), scales=scales[:], in_=h_packed[first][:])
            for e in range(first, end):
                h_words[e] = words[:, columns(e, first)]
                h_scales[e] = scales[:, columns(e, first)]

        def second_product(e, half, sums):
            nc.tensor.matmul_mx(
                out=sums,
                lhsT=w2[e][:, 2 * P * half : 2 * P * (half + 1)].bitcast(FP4X4),
                lhsT_scale=s2[e][:, P * half : P * (half + 1)],
                rhs=h_words[e].bitcast(FP8X4),
                rhs_scale=h_scales[e],
                start=True,
                stop=True,
            )

        turned_in = {end + 2: j for j, (first, end) in enumerate(TURNED[: EARLY_PACKS + 1])}
        packed_in = {end + 3: j for j, (first, end) in enumerate(TURNED[:EARLY_PACKS])}
        for step in range(E + 2):
            for stage, lag in ((multiply, 2), (activate, 1)):
                if 0 <= step - lag < E:
                    stage(step - lag)
            if step - 2 == 4:
                gather(*LATE_GATHER, "gelu_a4", "gelu_a3")
            if step in turned_in:
                turn(turned_in[step])
            if step in packed_in:
                pack(packed_in[step])
            if step < E - 1:
                w1_product(step)
            if step == E - 2:
                w1_product(E - 1)
            if step < E:
                w3_product(step)
        pack(EARLY_PACKS)
        for j in range(EARLY_PACKS + 1, len(TURNED)):
            turn(j)
            pack(j)
        for first, end in QUANTISED:
            quantise(first, end)
        for number, (first, end) in zip(result_bank, RESULTS):
            y_run[first] = bank(number, [P, (end - first) * C])
            for e in range(first, end):
                second_product(e, 0, y_run[first][:, columns(e, first)])
        for run, (first, end) in enumerate(RESULTS):
            copy = nc.vector.tensor_copy if run % 2 else nc.scalar.copy
            copy(out=y[0][:, first * C : end * C], in_=y_run[first][:])

        late_firsts = (0, LATE_RUN, E - LATE_RUN)
        late_banks = (bank_a(9), bank_a(10), bank_a(11))
        for first, number in zip(late_firsts, late_banks):
            late = bank(number, [P, LATE_RUN * C])
            for member in range(first, first + LATE_RUN):
                second_product(member, 1, late[:, columns(member, first)])
            nc.scalar.copy(out=y[1][:, first * C : (first + LATE_RUN) * C], in_=late[:])

        sum_banks = (result_bank[:BLOCKS], late_banks)
        back_banks = (result_bank[BLOCKS], bank_a(8))
        weighted, turned_sum, three, plain = {}, {}, {}, {}

        def fetch(r, half, first=0, end=T):
            if first == 0:
                name = f"weighted{half}{r}"
                weighted[half, r] = keep.tile([P, T], F32, name=name, align_bytes=64)
            entries = pos_t[r][:, first // PER_COLUMN : end // PER_COLUMN]
            nc.vector.tensor_tensor(
                weighted[half, r][:, first:end], y[half][:].indirect(entries), gates[r][:, first:end], MULT
            )

        def fetch_plain(r, half):
            name = f"plain{half}{r % 2}"
            plain[half, r] = keep.tile([P, T], F32, name=name, align_bytes=64)
            nc.scalar.activation(plain[half, r][:], y[half][:].indirect(pos_t[r][:]), COPY)

        def weigh(r, half):
            weighted[half, r] = keep.tile([P, T], F32, name=f"weighted{half}{r}", align_bytes=64)
            nc.vector.tensor_tensor(weighted[half, r][:], plain[half, r][:], gates[r], MULT)

        def add_turned(r, half):
            for b in range(BLOCKS):
                if r == SUMMED[half][0]:
                    turned_sum[half, b] = bank(sum_banks[half][b], [P, P])
                nc.tensor.matmul(
                    turned_sum[half, b][:],
                    lhsT=weighted[half, r][:, b * P : (b + 1) * P],
                    rhs=ident[:],
                    is_transpose=True,
                    start=(r == SUMMED[half][0]),
                    stop=(r == SUMMED[half][-1]),
                )

        staged = {}

        def stage(half):
            for b in range(BLOCKS):
                staged[half, b] = keep.tile([P, P], F32, name=f"staged{half}{b}", align_bytes=64)
                nc.scalar.copy(out=staged[half, b][:], in_=turned_sum[half, b][:])

        def turn_back(half):
            three[half] = bank(back_banks[half], [P, T])
            for b in range(BLOCKS):
                nc.tensor.transpose(three[half][:, b * P : (b + 1) * P], staged[half, b][:], ident[:])

        for r in SUMMED[1][1:]:
            fetch_plain(r, 1)
        for half in range(HALVES):
            for r in SUMMED[half]:
                if (half, r) in plain:
                    weigh(r, half)
                else:
                    fetch(r, half)
                add_turned(r, half)
            if half == 0:
                stage(0)
        fetch_plain(ADDED[1], 1)
        turn_back(0)
        stage(1)
        turn_back(1)
        pieces = ([(0, T)], [(0, T - P), (T - P, T)])
        total = [keep.tile([P, T], F32, name=f"total{half}", align_bytes=64) for half in range(HALVES)]

        def finish(half):
            for first, end in pieces[half]:
                nc.vector.tensor_tensor(
                    total[half][:, first:end], three[half][:, first:end], weighted[half, ADDED[half]][:, first:end], ADD
                )
                nc.sync.dma_start(out=out[half * P : (half + 1) * P, first:end], in_=total[half][:, first:end])

        fetch(ADDED[0], 0)
        weigh(ADDED[1], 1)
        finish(0)
        finish(1)
